import numpy as np
import ml_dtypes


def mxq(x, axis, fmt="e4m3"):
    dtype, down = {"e4m3": (ml_dtypes.float8_e4m3fn, 7), "e5m2": (ml_dtypes.float8_e5m2, 14)}[fmt]
    v = np.moveaxis(np.asarray(x, np.float32).astype(ml_dtypes.bfloat16).astype(np.float64), axis, -1)
    blocks = v.reshape(v.shape[:-1] + (-1, 32))
    amax = np.abs(blocks).max(-1, keepdims=True)
    byte = np.maximum(np.where(amax > 0, np.frexp(amax)[1] - 1 + 127, 0) - down, 1)
    scale = np.exp2(byte - 127.0)
    codes = (blocks / scale).astype(np.float32).astype(dtype).astype(np.float64)
    return np.moveaxis((codes * scale).reshape(v.shape), -1, axis)


WIDE = False


def mx_kscale(k):
    if not WIDE:
        return np.ones(k)
    levels = np.array([10, -10, 5, -5, 0])
    if k % 512:
        return np.exp2(np.random.permutation(np.resize(levels, k // 32))).repeat(32)
    a = np.empty((k // 512, 16))
    for p in range(k // 512):
        a[p, :8] = np.random.permutation(np.resize(levels, 8))
        for g in range(8):
            far = levels[np.abs(levels - a[p, g]) >= 10]
            a[p, g + 8] = far[np.random.randint(len(far))]
    return np.exp2(a.ravel()).repeat(32)


def f64(x):
    return np.asarray(x).astype(np.float64)


def striped(idx):
    return np.tile(idx.reshape(-1, 16).T, (8, 1)).astype(np.uint16)


def unstriped(offs):
    return offs[:16].T.reshape(-1).astype(np.int64)


E2M1 = np.array([0.0, 0.5, 1.0, 1.5, 2.0, 3.0, 4.0, 6.0, -0.0, -0.5, -1.0, -1.5, -2.0, -3.0, -4.0, -6.0])


def pack_weight(w, fmt):
    k, n = w.shape
    w = f64(np.asarray(w, np.float32).astype(ml_dtypes.bfloat16)).reshape(k // 32, 32, n)
    amax = np.abs(w).max(1)
    if fmt == "e4m3":
        byte = np.frexp(amax)[1] - 1 + 127 - 7
    else:
        mant, ex = np.frexp(amax / 6.0)
        byte = np.where(mant > 0.5, ex, ex - 1) + 127
    byte = np.clip(np.where(amax > 0, byte, 1), 1, 254)
    scaled = (w * np.exp2(127.0 - byte)[:, None, :]).reshape(k, n).astype(np.float32)
    by_word = np.ascontiguousarray(scaled.reshape(k // 512, 128, 4, n).transpose(0, 1, 3, 2))
    if fmt == "e4m3":
        words = by_word.astype(ml_dtypes.float8_e4m3fn).view(np.uint8)
    else:
        c = by_word.astype(ml_dtypes.float4_e2m1fn).view(np.uint8) & 0xF
        words = (c[..., 0::2] | (c[..., 1::2] << 4)).reshape(k // 512, 128, 2 * n)
    return np.ascontiguousarray(words), np.ascontiguousarray(byte.astype(np.uint8).reshape(k // 512, 16, n))


def unpack_weight(words, scales, fmt):
    g, _, n = scales.shape
    words = np.ascontiguousarray(words).reshape(g, 128, n, -1)
    if fmt == "e4m3":
        vals = words.view(ml_dtypes.float8_e4m3fn).astype(np.float64)
    else:
        nib = np.empty((g, 128, n, 4), np.uint8)
        nib[..., 0::2] = words & 0xF
        nib[..., 1::2] = words >> 4
        vals = E2M1[nib]
    vals = vals * np.repeat(np.exp2(scales.astype(np.float64) - 127.0), 8, axis=1)[..., None]
    return vals.transpose(0, 1, 3, 2).reshape(g * 512, n)


def gelu(v):
    return 0.5 * v * (1.0 + np.tanh(np.sqrt(2.0 / np.pi) * (v + 0.044715 * v**3)))


def striped8(idx):
    return np.concatenate([v.reshape(-1, 16).T for v in idx]).astype(np.uint16)


def unstriped8(offs):
    return np.stack([offs[16 * g:16 * g + 16].T.reshape(-1) for g in range(8)]).astype(np.int64)


def heads(xT, wgt, idx8):
    k = np.arange(xT.shape[0])
    return wgt[k // 4 % 128] * xT[k[:, None], idx8[k % 512 // 64]]


K, C, H, N, T, E, S = 512, 1024, 1024, 384, 2048, 2048, 1024

def setup_inputs():
    n = np.random.standard_normal
    s = mx_kscale(K)[:, None]
    sc = mx_kscale(C)[:, None]
    u = mx_kscale(H)[:, None]
    tab_words, tab_scales = pack_weight(n((C, T)) * sc, "e4m3")
    we_words, we_scales = pack_weight(n((C, H)) / np.sqrt(C) / sc * u.T, "e2m1")
    wp = n((K, H)) / np.sqrt(K) / s * np.sqrt(u).T
    return {
        "xT": (n((K, E)) * s).astype(np.float32),
        "wgt": np.repeat(np.random.uniform(0.5, 2.0, (8, S)), 16, axis=0).astype(np.float32),
        "offs2": striped8(np.stack([np.random.permutation(E)[:S] for _ in range(8)])),
        "tab_words": tab_words, "tab_scales": tab_scales,
        "offs": striped(np.random.permutation(T)[:S]),
        "wp": wp.astype(np.float32),
        "we_words": we_words, "we_scales": we_scales,
        "wf": (n((H, N)) / np.sqrt(H) / u).astype(np.float32),
        "load": (0.5 * n(N)).astype(np.float32),
    }

def reference(xT, wgt, offs2, tab_words, tab_scales, offs, wp, we_words, we_scales, wf, load):
    xg = mxq(heads(f64(xT), f64(wgt), unstriped8(offs2)), 0, "e4m3")
    v = unpack_weight(tab_words, tab_scales, "e4m3")[:, unstriped(offs)]
    we = unpack_weight(we_words, we_scales, "e2m1")
    p = mxq(f64(wp), 0, "e4m3").T @ xg
    e = we.T @ v
    h = np.maximum(np.square(p) - e, 0.0)
    y = mxq(f64(wf), 0, "e4m3").T @ mxq(h, 0, "e4m3")
    return y + f64(load)[:, None]

@@ -1,0 +1,303 @@
+from contextlib import ExitStack
+
+import concourse.mybir as mybir
+
+K, C, H, N, T, E, S = 512, 1024, 1024, 384, 2048, 2048, 1024
+FLOPS = 2 * S * (K * H + C * H + H * N)
+
+F32 = mybir.dt.float32
+BF16 = mybir.dt.bfloat16
+I32 = mybir.dt.int32
+U32 = mybir.dt.uint32
+U16 = mybir.dt.uint16
+U8 = mybir.dt.uint8
+FP8X4 = mybir.dt.float8_e4m3fn_x4
+FP4X4 = mybir.dt.float4_e2m1fn_x4
+ALU = mybir.AluOpType
+ACT = mybir.ActivationFunctionType
+
+P = 128
+PACK = 4
+PASS = P * PACK
+C_PASSES = C // PASS
+H_PASSES = H // PASS
+N_SLICES = N // P
+QUARTERS = 4
+QW = S // QUARTERS
+CHUNKS = QW // P
+LIST_COLS = QW // 16
+LAG = 3
+
+
+def tile_list_mesh_plastic_force_kernel(
+    tc, xT, wgt, offs2, tab_words, tab_scales, offs, wp, we_words, we_scales, wf, load, out
+):
+    nc = tc.nc
+    with ExitStack() as ctx:
+        keep = ctx.enter_context(tc.tile_pool(name="keep", bufs=1))
+        p_pool = ctx.enter_context(tc.psum_pool(name="p_psum", bufs=2))
+        e_pool = ctx.enter_context(tc.psum_pool(name="e_psum", bufs=3))
+        y_pool = ctx.enter_context(tc.psum_pool(name="y_psum", bufs=3))
+
+        def tile(name, shape, dtype):
+            return keep.tile(shape, dtype, name=name, align_bytes=64)
+
+        edge_list = tile("edge_list", [P, S // 16], U16)
+        tab_list = tile("tab_list", [P, S // 16], U16)
+        wgt_sb = tile("wgt_sb", [P, S], F32)
+        x_plane = [tile("x_plane%d" % i, [P, E], F32) for i in range(PACK)]
+        tab_w = [tile("tab_w%d" % a, [P, T], I32) for a in range(C_PASSES)]
+        tab_s = tile("tab_s", [P, T], U8)
+        picked_s = tile("picked_s", [P, S], U8)
+        v_codes = [tile("v_codes%d" % a, [P, S], U32) for a in range(C_PASSES)]
+        v_scales = [tile("v_scales%d" % a, [P, S], U8) for a in range(C_PASSES)]
+        we_raw = tile("we_raw", [P, C_PASSES, H // 2], I32)
+        we_s_raw = tile("we_s_raw", [P, C_PASSES, H // 4], I32)
+        we_codes = [tile("we_codes%d" % g, [P, C_PASSES * PASS * 2], U8) for g in range(H_PASSES)]
+        we_sc = [tile("we_sc%d" % g, [P, C_PASSES * PASS], U8) for g in range(H_PASSES)]
+        wp_raw = [tile("wp_raw%d" % g, [P, PACK, PASS], F32) for g in range(H_PASSES)]
+        wp_bf = [tile("wp_bf%d" % g, [P, PASS * PACK], BF16) for g in range(H_PASSES)]
+        wp_codes = [tile("wp_codes%d" % g, [P, PASS], U32) for g in range(H_PASSES)]
+        wp_sc = [tile("wp_sc%d" % g, [P, PASS], U8) for g in range(H_PASSES)]
+        wf_raw = [tile("wf_raw%d" % g, [P, PACK, N], F32) for g in range(H_PASSES)]
+        wf_bf = tile("wf_bf", [P, H_PASSES * N * PACK], BF16)
+        wf_codes = tile("wf_codes", [P, H_PASSES * N], U32)
+        wf_sc = tile("wf_sc", [P, H_PASSES * N], U8)
+        xg = [tile("xg%d" % q, [P, PACK, QW], F32) for q in range(QUARTERS)]
+        xg_bf = [tile("xg_bf%d" % q, [P, QW * PACK], BF16) for q in range(QUARTERS)]
+        xg_codes = [tile("xg_codes%d" % q, [P, QW], U32) for q in range(QUARTERS)]
+        xg_sc = [tile("xg_sc%d" % q, [P, QW], U8) for q in range(QUARTERS)]
+        bias = tile("bias", [P, N_SLICES], F32)
+        units = sorted(
+            [(q, g) for q in range(QUARTERS) for g in range(H_PASSES)],
+            key=lambda u: (u[0] + LAG * u[1], -u[1]),
+        )
+        sq = {u: tile("sq%d_%d" % u, [P, QW * PACK], F32) for u in units}
+        h_bf = {u: tile("h_bf%d_%d" % u, [P, QW * PACK], BF16) for u in units}
+        h_codes = {u: tile("h_codes%d_%d" % u, [P, QW], U32) for u in units}
+        h_sc = {u: tile("h_sc%d_%d" % u, [P, QW], U8) for u in units}
+        y_sb = [tile("y_sb%d" % q, [P, N_SLICES, QW], F32) for q in range(QUARTERS)]
+
+        nc.vector.memset(we_s_raw[:], 0)
+        nc.vector.memset(tab_s[32:64, :].bitcast(I32), 0)
+        nc.vector.memset(tab_s[64:128, :].bitcast(I32), 0)
+        for a in range(C_PASSES):
+            nc.vector.memset(v_scales[a][:].bitcast(I32), 0)
+
+        x_rows = xT.rearrange("(p i) e -> i p e", i=PACK)
+
+        def load_tab(a):
+            nc.sync.dma_start(
+                out=tab_w[a][:], in_=tab_words[a].rearrange("p t i -> p (t i)").bitcast(I32)
+            )
+
+        def load_wp(g):
+            nc.sync.dma_start(
+                out=wp_raw[g][:],
+                in_=wp[:, g * PASS : (g + 1) * PASS].rearrange("(p j) c -> p j c", j=PACK),
+            )
+
+        nc.sync.dma_start(
+            out=tab_s[0:32, :].bitcast(I32),
+            in_=tab_scales.rearrange("a q t -> (a q) t").bitcast(I32),
+        )
+        nc.sync.dma_start(out=tab_list[:], in_=offs)
+        nc.sync.dma_start(out=edge_list[:], in_=offs2)
+        nc.sync.dma_start(out=wgt_sb[:], in_=wgt)
+        nc.sync.dma_start(out=x_plane[0][:], in_=x_rows[0])
+        load_wp(0)
+        for quad in range(4):
+            nc.sync.dma_start(
+                out=we_s_raw[32 * quad : 32 * quad + 4, :, :],
+                in_=we_scales[:, 4 * quad : 4 * quad + 4, :].rearrange("a r n -> r a n").bitcast(I32),
+            )
+        for i in range(1, PACK):
+            nc.sync.dma_start(out=x_plane[i][:], in_=x_rows[i])
+        load_tab(0)
+        nc.sync.dma_start(out=we_raw[:], in_=we_words.rearrange("a p n -> p a n").bitcast(I32))
+        load_tab(1)
+        load_wp(1)
+        for g in range(H_PASSES):
+            wf_rows = wf[g * PASS : (g + 1) * PASS, :].rearrange("(b t i) n -> t b i n", t=PACK, i=8)
+            for t in range(PACK):
+                nc.sync.dma_start(out=wf_raw[g][:, t, :], in_=wf_rows[t])
+        with nc.allow_non_contiguous_dma(reason="one bias value a partition"):
+            nc.gpsimd.dma_start(out=bias[:], in_=load.rearrange("(s p) -> p s", p=P))
+
+        def qcols(q):
+            return slice(q * QW, (q + 1) * QW)
+
+        def qlist(lst, q):
+            return lst[:, q * LIST_COLS : (q + 1) * LIST_COLS]
+
+        def gather_x(i, q):
+            nc.vector.tensor_tensor(
+                xg[q][:, i, :], x_plane[i][:].indirect(qlist(edge_list, q)), wgt_sb[:, qcols(q)], ALU.mult
+            )
+
+        def weave_x(q):
+            nc.scalar.activation(
+                out=xg_bf[q][:].rearrange("p (c i t) -> p c t i", i=4, t=PACK),
+                in_=xg[q][:].rearrange("p t (c i) -> p c t i", i=4),
+                func=ACT.Copy,
+            )
+
+        def quantize(codes, scales, values):
+            nc.vector.quantize_mx(out=codes.bitcast(FP8X4), scales=scales, in_=values)
+
+        def weave_wp(g, t):
+            nc.scalar.activation(
+                out=wp_bf[g][:, t * PASS : (t + 1) * PASS].rearrange("p (b i j) -> p b j i", i=8, j=PACK),
+                in_=wp_raw[g][:].rearrange("p j (b t i) -> p t b j i", t=PACK, i=8)[:, t],
+                func=ACT.Copy,
+            )
+
+        def prepare_wp(g):
+            for t in range(PACK):
+                weave_wp(g, t)
+            quantize(wp_codes[g][:], wp_sc[g][:], wp_bf[g][:])
+
+        def weave_wf(g, s):
+            lo = (g * N + s * P) * PACK
+            nc.scalar.activation(
+                out=wf_bf[:, lo : lo + P * PACK].rearrange("p (c i t) -> p c t i", i=4, t=PACK),
+                in_=wf_raw[g][:, :, s * P : (s + 1) * P].rearrange("p t (c i) -> p c t i", i=4),
+                func=ACT.Copy,
+            )
+
+        def order_we(g):
+            nc.vector.tensor_copy(
+                out=we_codes[g][:].bitcast(I32).rearrange("p (a t b w) -> p a t b w", a=C_PASSES, t=PACK, w=4),
+                in_=we_raw[:, :, g * 256 : (g + 1) * 256].rearrange("p a (b t w) -> p a t b w", t=PACK, w=4),
+            )
+            nc.vector.tensor_copy(
+                out=we_sc[g][:].bitcast(I32).rearrange("p (a t b w) -> p a t b w", a=C_PASSES, t=PACK, w=2),
+                in_=we_s_raw[:, :, g * 128 : (g + 1) * 128].rearrange("p a (b t w) -> p a t b w", t=PACK, w=2),
+            )
+
+        def gather_tab(a, lo, hi):
+            nc.vector.tensor_copy(
+                v_codes[a][:, lo * QW : hi * QW],
+                tab_w[a][:].bitcast(U32).indirect(tab_list[:, lo * LIST_COLS : hi * LIST_COLS]),
+            )
+
+        def square(u):
+            q, g = u
+            for c in range(CHUNKS):
+                bank = p_pool.tile([P, PACK, P], F32, name="p_bank")
+                cols = slice(c * P, (c + 1) * P)
+                for t in range(PACK):
+                    w = slice(t * P, (t + 1) * P)
+                    nc.tensor.matmul_mx(
+                        out=bank[:, t, :],
+                        lhsT=wp_codes[g][:, w].bitcast(FP8X4),
+                        lhsT_scale=wp_sc[g][:, w],
+                        rhs=xg_codes[q][:, cols].bitcast(FP8X4),
+                        rhs_scale=xg_sc[q][:, cols],
+                        start=True,
+                        stop=True,
+                    )
+                nc.scalar.activation(
+                    out=sq[u][:, c * PASS : (c + 1) * PASS].rearrange("p (n t) -> p n t", t=PACK),
+                    in_=bank[:].rearrange("p t n -> p n t"),
+                    func=ACT.Square,
+                )
+
+        def subtract(u, c):
+            q, g = u
+            bank = e_pool.tile([P, PACK, P], F32, name="e_bank")
+            cols = slice(q * QW + c * P, q * QW + (c + 1) * P)
+            for t in range(PACK):
+                for a in range(C_PASSES):
+                    lo = (a * PACK + t) * P
+                    nc.tensor.matmul_mx(
+                        out=bank[:, t, :],
+                        lhsT=we_codes[g][:, 2 * lo : 2 * (lo + P)].bitcast(FP4X4),
+                        lhsT_scale=we_sc[g][:, lo : lo + P],
+                        rhs=v_codes[a][:, cols].bitcast(FP8X4),
+                        rhs_scale=v_scales[a][:, cols],
+                        start=(a == 0),
+                        stop=(a == C_PASSES - 1),
+                    )
+            part = slice(c * PASS, (c + 1) * PASS)
+            nc.vector.tensor_tensor(
+                h_bf[u][:, part].rearrange("p (n t) -> p n t", t=PACK),
+                sq[u][:, part].rearrange("p (n t) -> p n t", t=PACK),
+                bank[:].rearrange("p t n -> p n t"),
+                ALU.subtract,
+            )
+
+        def clamp(u):
+            nc.vector.tensor_scalar_max(h_bf[u][:], h_bf[u][:], 0.0)
+
+        def force(q):
+            for s in range(N_SLICES):
+                bank = y_pool.tile([P, QW], F32, name="y_bank")
+                for g in range(H_PASSES):
+                    w = slice(g * N + s * P, g * N + (s + 1) * P)
+                    nc.tensor.matmul_mx(
+                        out=bank[:],
+                        lhsT=wf_codes[:, w].bitcast(FP8X4),
+                        lhsT_scale=wf_sc[:, w],
+                        rhs=h_codes[(q, g)][:].bitcast(FP8X4),
+                        rhs_scale=h_sc[(q, g)][:],
+                        start=(g == 0),
+                        stop=(g == H_PASSES - 1),
+                    )
+                nc.scalar.activation(
+                    out=y_sb[q][:, s, :], in_=bank[:], func=ACT.Identity, bias=bias[:, s : s + 1]
+                )
+            nc.sync.dma_start(
+                out=out.rearrange("(s p) j -> p s j", p=P)[:, :, qcols(q)], in_=y_sb[q][:]
+            )
+
+        def finish(u):
+            quantize(h_codes[u][:], h_sc[u][:], h_bf[u][:])
+            if u[1] == H_PASSES - 1:
+                force(u[0])
+
+        nc.vector.tensor_copy(picked_s[:], tab_s[:].indirect(tab_list[:]))
+        for a in range(C_PASSES):
+            for quad in range(4):
+                row = 16 * a + 4 * quad
+                (nc.gpsimd, nc.scalar)[a].dma_start(
+                    out=v_scales[a][32 * quad : 32 * quad + 4, :].bitcast(I32),
+                    in_=picked_s[row : row + 4, :].bitcast(I32),
+                )
+        for q in range(QUARTERS):
+            gather_x(0, q)
+        prepare_wp(0)
+        for i in range(1, PACK - 1):
+            for q in range(QUARTERS):
+                gather_x(i, q)
+        for q in range(QUARTERS):
+            gather_x(PACK - 1, q)
+            weave_x(q)
+        for q in range(QUARTERS):
+            quantize(xg_codes[q][:], xg_sc[q][:], xg_bf[q][:])
+            square((q, 0))
+        gather_tab(0, 0, QUARTERS)
+        order_we(0)
+        gather_tab(1, 0, 1)
+        prepare_wp(1)
+        for n, u in enumerate(units):
+            if u[1] == 0 and u[0] + 1 < QUARTERS:
+                gather_tab(1, u[0] + 1, u[0] + 2)
+            if u[1] == 1:
+                square(u)
+            if n == 1:
+                order_we(1)
+            if u == (0, 1):
+                for g in range(H_PASSES):
+                    for s in range(N_SLICES):
+                        weave_wf(g, s)
+                quantize(wf_codes[:, 0:512], wf_sc[:, 0:512], wf_bf[:, 0:2048])
+                quantize(wf_codes[:, 512:768], wf_sc[:, 512:768], wf_bf[:, 2048:3072])
+            subtract(u, 0)
+            if n > 0:
+                clamp(units[n - 1])
+            subtract(u, 1)
+            if n > 0:
+                finish(units[n - 1])
+        clamp(units[-1])
+        finish(units[-1])

@@ -19,6 +19,8 @@ ACT = mybir.ActivationFunctionType
 P = 128
 PACK = 4
 PASS = P * PACK
+RUN = 8
+QUADS = 4
 C_PASSES = C // PASS
 H_PASSES = H // PASS
 N_SLICES = N // P
@@ -26,7 +28,8 @@ QUARTERS = 4
 QW = S // QUARTERS
 CHUNKS = QW // P
 LIST_COLS = QW // 16
-LAG = 3
+P_BANKS, E_BANKS, Y_BANKS = 2, 3, N_SLICES
+WF_SPLIT = 512
 
 
 def tile_list_mesh_plastic_force_kernel(
@@ -35,12 +38,12 @@ def tile_list_mesh_plastic_force_kernel(
     nc = tc.nc
     with ExitStack() as ctx:
         keep = ctx.enter_context(tc.tile_pool(name="keep", bufs=1))
-        p_pool = ctx.enter_context(tc.psum_pool(name="p_psum", bufs=2))
-        e_pool = ctx.enter_context(tc.psum_pool(name="e_psum", bufs=3))
-        y_pool = ctx.enter_context(tc.psum_pool(name="y_psum", bufs=3))
+        p_pool = ctx.enter_context(tc.psum_pool(name="p_psum", bufs=P_BANKS))
+        e_pool = ctx.enter_context(tc.psum_pool(name="e_psum", bufs=E_BANKS))
+        y_pool = ctx.enter_context(tc.psum_pool(name="y_psum", bufs=Y_BANKS))
 
         def tile(name, shape, dtype):
-            return keep.tile(shape, dtype, name=name, align_bytes=64)
+            return keep.tile(shape, dtype, name=name, tag=name, align_bytes=64)
 
         edge_list = tile("edge_list", [P, S // 16], U16)
         tab_list = tile("tab_list", [P, S // 16], U16)
@@ -51,128 +54,122 @@ def tile_list_mesh_plastic_force_kernel(
         picked_s = tile("picked_s", [P, S], U8)
         v_codes = [tile("v_codes%d" % a, [P, S], U32) for a in range(C_PASSES)]
         v_scales = [tile("v_scales%d" % a, [P, S], U8) for a in range(C_PASSES)]
-        we_raw = tile("we_raw", [P, C_PASSES, H // 2], I32)
+        we_raw = [tile("we_raw%d" % g, [P, C_PASSES, PASS // 2], I32) for g in range(H_PASSES)]
         we_s_raw = tile("we_s_raw", [P, C_PASSES, H // 4], I32)
         we_codes = [tile("we_codes%d" % g, [P, C_PASSES * PASS * 2], U8) for g in range(H_PASSES)]
         we_sc = [tile("we_sc%d" % g, [P, C_PASSES * PASS], U8) for g in range(H_PASSES)]
-        wp_raw = [tile("wp_raw%d" % g, [P, PACK, PASS], F32) for g in range(H_PASSES)]
         wp_bf = [tile("wp_bf%d" % g, [P, PASS * PACK], BF16) for g in range(H_PASSES)]
         wp_codes = [tile("wp_codes%d" % g, [P, PASS], U32) for g in range(H_PASSES)]
         wp_sc = [tile("wp_sc%d" % g, [P, PASS], U8) for g in range(H_PASSES)]
-        wf_raw = [tile("wf_raw%d" % g, [P, PACK, N], F32) for g in range(H_PASSES)]
         wf_bf = tile("wf_bf", [P, H_PASSES * N * PACK], BF16)
         wf_codes = tile("wf_codes", [P, H_PASSES * N], U32)
         wf_sc = tile("wf_sc", [P, H_PASSES * N], U8)
-        xg = [tile("xg%d" % q, [P, PACK, QW], F32) for q in range(QUARTERS)]
+        xg = tile("xg", [P, PACK, S], F32)
         xg_bf = [tile("xg_bf%d" % q, [P, QW * PACK], BF16) for q in range(QUARTERS)]
         xg_codes = [tile("xg_codes%d" % q, [P, QW], U32) for q in range(QUARTERS)]
         xg_sc = [tile("xg_sc%d" % q, [P, QW], U8) for q in range(QUARTERS)]
         bias = tile("bias", [P, N_SLICES], F32)
-        units = sorted(
-            [(q, g) for q in range(QUARTERS) for g in range(H_PASSES)],
-            key=lambda u: (u[0] + LAG * u[1], -u[1]),
-        )
+        units = [(q, g) for g in range(H_PASSES) for q in range(QUARTERS)]
         sq = {u: tile("sq%d_%d" % u, [P, QW * PACK], F32) for u in units}
         h_bf = {u: tile("h_bf%d_%d" % u, [P, QW * PACK], BF16) for u in units}
         h_codes = {u: tile("h_codes%d_%d" % u, [P, QW], U32) for u in units}
         h_sc = {u: tile("h_sc%d_%d" % u, [P, QW], U8) for u in units}
         y_sb = [tile("y_sb%d" % q, [P, N_SLICES, QW], F32) for q in range(QUARTERS)]
-
-        nc.vector.memset(we_s_raw[:], 0)
-        nc.vector.memset(tab_s[32:64, :].bitcast(I32), 0)
-        nc.vector.memset(tab_s[64:128, :].bitcast(I32), 0)
-        for a in range(C_PASSES):
-            nc.vector.memset(v_scales[a][:].bitcast(I32), 0)
+        wp_raw = [tile("wp_raw%d" % g, [P, PACK, PASS], F32) for g in range(H_PASSES)]
+        wf_raw = [tile("wf_raw%d" % g, [P, PACK, N], F32) for g in range(H_PASSES)]
 
         x_rows = xT.rearrange("(p i) e -> i p e", i=PACK)
 
+        def load_wgt(half):
+            cols = slice(half * (S // 2), (half + 1) * (S // 2))
+            nc.sync.dma_start(out=wgt_sb[:, cols], in_=wgt[:, cols])
+
+        def load_x(i):
+            nc.sync.dma_start(out=x_plane[i][:], in_=x_rows[i])
+
         def load_tab(a):
-            nc.sync.dma_start(
-                out=tab_w[a][:], in_=tab_words[a].rearrange("p t i -> p (t i)").bitcast(I32)
-            )
+            nc.sync.dma_start(out=tab_w[a][:], in_=tab_words[a].rearrange("p t i -> p (t i)").bitcast(I32))
 
         def load_wp(g):
             nc.sync.dma_start(
-                out=wp_raw[g][:],
-                in_=wp[:, g * PASS : (g + 1) * PASS].rearrange("(p j) c -> p j c", j=PACK),
+                out=wp_raw[g][:], in_=wp[:, g * PASS : (g + 1) * PASS].rearrange("(p j) c -> p j c", j=PACK)
             )
 
-        nc.sync.dma_start(
-            out=tab_s[0:32, :].bitcast(I32),
-            in_=tab_scales.rearrange("a q t -> (a q) t").bitcast(I32),
-        )
-        nc.sync.dma_start(out=tab_list[:], in_=offs)
-        nc.sync.dma_start(out=edge_list[:], in_=offs2)
-        nc.sync.dma_start(out=wgt_sb[:], in_=wgt)
-        nc.sync.dma_start(out=x_plane[0][:], in_=x_rows[0])
-        load_wp(0)
-        for quad in range(4):
-            nc.sync.dma_start(
-                out=we_s_raw[32 * quad : 32 * quad + 4, :, :],
-                in_=we_scales[:, 4 * quad : 4 * quad + 4, :].rearrange("a r n -> r a n").bitcast(I32),
-            )
-        for i in range(1, PACK):
-            nc.sync.dma_start(out=x_plane[i][:], in_=x_rows[i])
-        load_tab(0)
-        nc.sync.dma_start(out=we_raw[:], in_=we_words.rearrange("a p n -> p a n").bitcast(I32))
-        load_tab(1)
-        load_wp(1)
-        for g in range(H_PASSES):
-            wf_rows = wf[g * PASS : (g + 1) * PASS, :].rearrange("(b t i) n -> t b i n", t=PACK, i=8)
+        def load_wf(g):
+            rows = wf[g * PASS : (g + 1) * PASS, :].rearrange("(b t i) n -> t b i n", t=PACK, i=RUN)
             for t in range(PACK):
-                nc.sync.dma_start(out=wf_raw[g][:, t, :], in_=wf_rows[t])
-        with nc.allow_non_contiguous_dma(reason="one bias value a partition"):
-            nc.gpsimd.dma_start(out=bias[:], in_=load.rearrange("(s p) -> p s", p=P))
+                nc.sync.dma_start(out=wf_raw[g][:, t, :], in_=rows[t])
 
-        def qcols(q):
-            return slice(q * QW, (q + 1) * QW)
-
-        def qlist(lst, q):
-            return lst[:, q * LIST_COLS : (q + 1) * LIST_COLS]
-
-        def gather_x(i, q):
-            nc.vector.tensor_tensor(
-                xg[q][:, i, :], x_plane[i][:].indirect(qlist(edge_list, q)), wgt_sb[:, qcols(q)], ALU.mult
+        def load_we(g):
+            nc.sync.dma_start(
+                out=we_raw[g][:],
+                in_=we_words[:, :, 2 * g * PASS : 2 * (g + 1) * PASS].rearrange("a p n -> p a n").bitcast(I32),
             )
 
-        def weave_x(q):
-            nc.scalar.activation(
-                out=xg_bf[q][:].rearrange("p (c i t) -> p c t i", i=4, t=PACK),
-                in_=xg[q][:].rearrange("p t (c i) -> p c t i", i=4),
-                func=ACT.Copy,
-            )
+        def load_we_scales():
+            for quad in range(QUADS):
+                nc.sync.dma_start(
+                    out=we_s_raw[32 * quad : 32 * quad + 4, :, :],
+                    in_=we_scales[:, 4 * quad : 4 * quad + 4, :].rearrange("a r n -> r a n").bitcast(I32),
+                )
+
+        def move_scales(a):
+            for quad in range(QUADS):
+                row = 16 * a + 4 * quad
+                nc.sync.dma_start(
+                    out=v_scales[a][32 * quad : 32 * quad + 4, :].bitcast(I32),
+                    in_=picked_s[row : row + 4, :].bitcast(I32),
+                )
 
         def quantize(codes, scales, values):
             nc.vector.quantize_mx(out=codes.bitcast(FP8X4), scales=scales, in_=values)
 
-        def weave_wp(g, t):
-            nc.scalar.activation(
-                out=wp_bf[g][:, t * PASS : (t + 1) * PASS].rearrange("p (b i j) -> p b j i", i=8, j=PACK),
-                in_=wp_raw[g][:].rearrange("p j (b t i) -> p t b j i", t=PACK, i=8)[:, t],
-                func=ACT.Copy,
+        def weave(dst, src):
+            nc.scalar.activation(out=dst, in_=src, func=ACT.Copy)
+
+        def gather_x(i, lo, hi):
+            nc.vector.tensor_tensor(
+                xg[:, i, lo * QW : hi * QW],
+                x_plane[i][:].indirect(edge_list[:, lo * LIST_COLS : hi * LIST_COLS]),
+                wgt_sb[:, lo * QW : hi * QW],
+                ALU.mult,
             )
+
+        def prepare_x(q):
+            weave(
+                xg_bf[q][:].rearrange("p (s t) -> p s t", t=PACK),
+                xg[:, :, q * QW : (q + 1) * QW].rearrange("p t s -> p s t"),
+            )
+            quantize(xg_codes[q][:], xg_sc[q][:], xg_bf[q][:])
 
         def prepare_wp(g):
             for t in range(PACK):
-                weave_wp(g, t)
+                weave(
+                    wp_bf[g][:, t * PASS : (t + 1) * PASS].rearrange("p (b i j) -> p b i j", i=RUN, j=PACK),
+                    wp_raw[g][:].rearrange("p j (b t i) -> p t b i j", t=PACK, i=RUN)[:, t],
+                )
             quantize(wp_codes[g][:], wp_sc[g][:], wp_bf[g][:])
 
-        def weave_wf(g, s):
-            lo = (g * N + s * P) * PACK
-            nc.scalar.activation(
-                out=wf_bf[:, lo : lo + P * PACK].rearrange("p (c i t) -> p c t i", i=4, t=PACK),
-                in_=wf_raw[g][:, :, s * P : (s + 1) * P].rearrange("p t (c i) -> p c t i", i=4),
-                func=ACT.Copy,
-            )
+        def prepare_wf():
+            for g in range(H_PASSES):
+                for s in range(N_SLICES):
+                    lo = (g * N + s * P) * PACK
+                    weave(
+                        wf_bf[:, lo : lo + P * PACK].rearrange("p (n t) -> p n t", t=PACK),
+                        wf_raw[g][:, :, s * P : (s + 1) * P].rearrange("p t n -> p n t"),
+                    )
+            for lo, hi in ((0, WF_SPLIT), (WF_SPLIT, H_PASSES * N)):
+                quantize(wf_codes[:, lo:hi], wf_sc[:, lo:hi], wf_bf[:, lo * PACK : hi * PACK])
 
         def order_we(g):
             nc.vector.tensor_copy(
                 out=we_codes[g][:].bitcast(I32).rearrange("p (a t b w) -> p a t b w", a=C_PASSES, t=PACK, w=4),
-                in_=we_raw[:, :, g * 256 : (g + 1) * 256].rearrange("p a (b t w) -> p a t b w", t=PACK, w=4),
+                in_=we_raw[g][:].rearrange("p a (b t w) -> p a t b w", t=PACK, w=4),
             )
+            words = PASS // 4
             nc.vector.tensor_copy(
                 out=we_sc[g][:].bitcast(I32).rearrange("p (a t b w) -> p a t b w", a=C_PASSES, t=PACK, w=2),
-                in_=we_s_raw[:, :, g * 128 : (g + 1) * 128].rearrange("p a (b t w) -> p a t b w", t=PACK, w=2),
+                in_=we_s_raw[:, :, g * words : (g + 1) * words].rearrange("p a (b t w) -> p a t b w", t=PACK, w=2),
             )
 
         def gather_tab(a, lo, hi):
@@ -227,77 +224,115 @@ def tile_list_mesh_plastic_force_kernel(
                 ALU.subtract,
             )
 
-        def clamp(u):
-            nc.vector.tensor_scalar_max(h_bf[u][:], h_bf[u][:], 0.0)
+        def clamp(u, lo, hi):
+            part = h_bf[u][:, lo * PACK : hi * PACK]
+            nc.vector.tensor_scalar_max(part, part, 0.0)
 
-        def force(q):
+        def force(q, lo, hi):
+            last = q == QUARTERS - 1 and hi == QW
             for s in range(N_SLICES):
-                bank = y_pool.tile([P, QW], F32, name="y_bank")
+                if last and s < P_BANKS:
+                    bank = p_pool.tile([P, hi - lo], F32, name="p_bank")
+                else:
+                    bank = y_pool.tile([P, hi - lo], F32, name="y_bank")
                 for g in range(H_PASSES):
                     w = slice(g * N + s * P, g * N + (s + 1) * P)
                     nc.tensor.matmul_mx(
                         out=bank[:],
                         lhsT=wf_codes[:, w].bitcast(FP8X4),
                         lhsT_scale=wf_sc[:, w],
-                        rhs=h_codes[(q, g)][:].bitcast(FP8X4),
-                        rhs_scale=h_sc[(q, g)][:],
+                        rhs=h_codes[(q, g)][:, lo:hi].bitcast(FP8X4),
+                        rhs_scale=h_sc[(q, g)][:, lo:hi],
                         start=(g == 0),
                         stop=(g == H_PASSES - 1),
                     )
-                nc.scalar.activation(
-                    out=y_sb[q][:, s, :], in_=bank[:], func=ACT.Identity, bias=bias[:, s : s + 1]
-                )
+                if last and s % 2 == 0:
+                    nc.vector.tensor_scalar_add(y_sb[q][:, s, lo:hi], bank[:], bias[:, s : s + 1])
+                else:
+                    nc.scalar.activation(
+                        out=y_sb[q][:, s, lo:hi], in_=bank[:], func=ACT.Identity, bias=bias[:, s : s + 1]
+                    )
             nc.sync.dma_start(
-                out=out.rearrange("(s p) j -> p s j", p=P)[:, :, qcols(q)], in_=y_sb[q][:]
+                out=out.rearrange("(s p) j -> p s j", p=P)[:, :, q * QW + lo : q * QW + hi],
+                in_=y_sb[q][:, :, lo:hi],
             )
 
-        def finish(u):
-            quantize(h_codes[u][:], h_sc[u][:], h_bf[u][:])
-            if u[1] == H_PASSES - 1:
-                force(u[0])
+        def finish(u, lo, hi):
+            q, g = u
+            quantize(h_codes[u][:, lo:hi], h_sc[u][:, lo:hi], h_bf[u][:, lo * PACK : hi * PACK])
+            if g == H_PASSES - 1:
+                force(q, lo, hi)
 
-        nc.vector.tensor_copy(picked_s[:], tab_s[:].indirect(tab_list[:]))
+        nc.vector.memset(we_s_raw[:], 0)
+        nc.vector.memset(tab_s[32:64, :].bitcast(I32), 0)
+        nc.vector.memset(tab_s[64:128, :].bitcast(I32), 0)
         for a in range(C_PASSES):
-            for quad in range(4):
-                row = 16 * a + 4 * quad
-                (nc.gpsimd, nc.scalar)[a].dma_start(
-                    out=v_scales[a][32 * quad : 32 * quad + 4, :].bitcast(I32),
-                    in_=picked_s[row : row + 4, :].bitcast(I32),
-                )
-        for q in range(QUARTERS):
-            gather_x(0, q)
-        prepare_wp(0)
+            nc.vector.memset(v_scales[a][:].bitcast(I32), 0)
+
+        nc.sync.dma_start(
+            out=tab_s[0:32, :].bitcast(I32), in_=tab_scales.rearrange("a q t -> (a q) t").bitcast(I32)
+        )
+        nc.sync.dma_start(out=tab_list[:], in_=offs)
+        nc.vector.tensor_copy(picked_s[:], tab_s[:].indirect(tab_list[:]))
+        nc.sync.dma_start(out=edge_list[:], in_=offs2)
+
+        load_wgt(0)
+        load_x(0)
+        load_wgt(1)
+        load_x(1)
+        load_x(2)
+        load_wp(0)
+        load_x(3)
+        load_we_scales()
+        load_tab(0)
+        load_we(0)
+        move_scales(0)
+        load_tab(1)
+        move_scales(1)
+        load_wp(1)
+        load_we(1)
+        for g in range(H_PASSES):
+            load_wf(g)
+        with nc.allow_non_contiguous_dma(reason="one bias value a partition"):
+            nc.sync.dma_start(out=bias[:], in_=load.rearrange("(s p) -> p s", p=P))
+
+        for half in range(2):
+            gather_x(0, 2 * half, 2 * half + 2)
         for i in range(1, PACK - 1):
-            for q in range(QUARTERS):
-                gather_x(i, q)
+            gather_x(i, 0, QUARTERS)
+        prepare_wp(0)
         for q in range(QUARTERS):
-            gather_x(PACK - 1, q)
-            weave_x(q)
+            gather_x(PACK - 1, q, q + 1)
         for q in range(QUARTERS):
-            quantize(xg_codes[q][:], xg_sc[q][:], xg_bf[q][:])
+            prepare_x(q)
             square((q, 0))
-        gather_tab(0, 0, QUARTERS)
+        gather_tab(0, 0, 2)
         order_we(0)
         gather_tab(1, 0, 1)
+        gather_tab(0, 2, QUARTERS)
         prepare_wp(1)
+
         for n, u in enumerate(units):
-            if u[1] == 0 and u[0] + 1 < QUARTERS:
-                gather_tab(1, u[0] + 1, u[0] + 2)
-            if u[1] == 1:
-                square(u)
+            q, g = u
+            if g == 0 and q + 1 < QUARTERS:
+                gather_tab(1, q + 1, q + 2)
             if n == 1:
                 order_we(1)
+            if QUARTERS <= n + 1 < len(units):
+                square(units[n + 1])
             if u == (0, 1):
-                for g in range(H_PASSES):
-                    for s in range(N_SLICES):
-                        weave_wf(g, s)
-                quantize(wf_codes[:, 0:512], wf_sc[:, 0:512], wf_bf[:, 0:2048])
-                quantize(wf_codes[:, 512:768], wf_sc[:, 512:768], wf_bf[:, 2048:3072])
+                prepare_wf()
             subtract(u, 0)
             if n > 0:
-                clamp(units[n - 1])
-            subtract(u, 1)
-            if n > 0:
-                finish(units[n - 1])
-        clamp(units[-1])
-        finish(units[-1])
+                clamp(units[n - 1], 0, QW)
+            if n + 1 < len(units):
+                subtract(u, 1)
+                if n > 0:
+                    finish(units[n - 1], 0, QW)
+        u = units[-1]
+        finish(units[-2], 0, QW)
+        clamp(u, 0, P)
+        subtract(u, 1)
+        finish(u, 0, P)
+        clamp(u, P, QW)
+        finish(u, P, QW)

@@ -20,6 +20,8 @@ P = 128
 PACK = 4
 PASS = P * PACK
 RUN = 8
+LINE = 4
+PAIR = 2
 QUADS = 4
 C_PASSES = C // PASS
 H_PASSES = H // PASS
@@ -137,16 +139,16 @@ def tile_list_mesh_plastic_force_kernel(
 
         def prepare_x(q):
             weave(
-                xg_bf[q][:].rearrange("p (s t) -> p s t", t=PACK),
-                xg[:, :, q * QW : (q + 1) * QW].rearrange("p t s -> p s t"),
+                xg_bf[q][:].rearrange("p (c i t) -> p c t i", i=LINE, t=PACK),
+                xg[:, :, q * QW : (q + 1) * QW].rearrange("p t (c i) -> p c t i", i=LINE),
             )
             quantize(xg_codes[q][:], xg_sc[q][:], xg_bf[q][:])
 
         def prepare_wp(g):
             for t in range(PACK):
                 weave(
-                    wp_bf[g][:, t * PASS : (t + 1) * PASS].rearrange("p (b i j) -> p b i j", i=RUN, j=PACK),
-                    wp_raw[g][:].rearrange("p j (b t i) -> p t b i j", t=PACK, i=RUN)[:, t],
+                    wp_bf[g][:, t * PASS : (t + 1) * PASS].rearrange("p (b i j) -> p b j i", i=RUN, j=PACK),
+                    wp_raw[g][:].rearrange("p j (b t i) -> p t b j i", t=PACK, i=RUN)[:, t],
                 )
             quantize(wp_codes[g][:], wp_sc[g][:], wp_bf[g][:])
 
@@ -155,8 +157,8 @@ def tile_list_mesh_plastic_force_kernel(
                 for s in range(N_SLICES):
                     lo = (g * N + s * P) * PACK
                     weave(
-                        wf_bf[:, lo : lo + P * PACK].rearrange("p (n t) -> p n t", t=PACK),
-                        wf_raw[g][:, :, s * P : (s + 1) * P].rearrange("p t n -> p n t"),
+                        wf_bf[:, lo : lo + P * PACK].rearrange("p (c i t) -> p c t i", i=LINE, t=PACK),
+                        wf_raw[g][:, :, s * P : (s + 1) * P].rearrange("p t (c i) -> p c t i", i=LINE),
                     )
             for lo, hi in ((0, WF_SPLIT), (WF_SPLIT, H_PASSES * N)):
                 quantize(wf_codes[:, lo:hi], wf_sc[:, lo:hi], wf_bf[:, lo * PACK : hi * PACK])
@@ -195,8 +197,8 @@ def tile_list_mesh_plastic_force_kernel(
                         stop=True,
                     )
                 nc.scalar.activation(
-                    out=sq[u][:, c * PASS : (c + 1) * PASS].rearrange("p (n t) -> p n t", t=PACK),
-                    in_=bank[:].rearrange("p t n -> p n t"),
+                    out=sq[u][:, c * PASS : (c + 1) * PASS].rearrange("p (n t i) -> p n t i", t=PACK, i=PAIR),
+                    in_=bank[:].rearrange("p t (n i) -> p n t i", i=PAIR),
                     func=ACT.Square,
                 )
 
@@ -218,9 +220,9 @@ def tile_list_mesh_plastic_force_kernel(
                     )
             part = slice(c * PASS, (c + 1) * PASS)
             nc.vector.tensor_tensor(
-                h_bf[u][:, part].rearrange("p (n t) -> p n t", t=PACK),
-                sq[u][:, part].rearrange("p (n t) -> p n t", t=PACK),
-                bank[:].rearrange("p t n -> p n t"),
+                h_bf[u][:, part].rearrange("p (n i t) -> p n t i", t=PACK, i=PAIR),
+                sq[u][:, part].rearrange("p (n t i) -> p n t i", t=PACK, i=PAIR),
+                bank[:].rearrange("p t (n i) -> p n t i", i=PAIR),
                 ALU.subtract,
             )
 

@@ -1,6 +1,7 @@
 from contextlib import ExitStack
 
 import concourse.mybir as mybir
+from concourse.masks import make_identity
 
 K, C, H, N, T, E, S = 512, 1024, 1024, 384, 2048, 2048, 1024
 FLOPS = 2 * S * (K * H + C * H + H * N)
@@ -20,7 +21,7 @@ P = 128
 PACK = 4
 PASS = P * PACK
 RUN = 8
-LINE = 4
+LINE = 2
 PAIR = 2
 QUADS = 4
 C_PASSES = C // PASS
@@ -50,6 +51,9 @@ def tile_list_mesh_plastic_force_kernel(
         edge_list = tile("edge_list", [P, S // 16], U16)
         tab_list = tile("tab_list", [P, S // 16], U16)
         wgt_sb = tile("wgt_sb", [P, S], F32)
+        wgt_rows = tile("wgt_rows", [P, P], F32)
+        wgt_turned = tile("wgt_turned", [P, S // P, P], F32)
+        ident = tile("ident", [P, P], F32)
         x_plane = [tile("x_plane%d" % i, [P, E], F32) for i in range(PACK)]
         tab_w = [tile("tab_w%d" % a, [P, T], I32) for a in range(C_PASSES)]
         tab_s = tile("tab_s", [P, T], U8)
@@ -82,9 +86,26 @@ def tile_list_mesh_plastic_force_kernel(
 
         x_rows = xT.rearrange("(p i) e -> i p e", i=PACK)
 
-        def load_wgt(half):
-            cols = slice(half * (S // 2), (half + 1) * (S // 2))
-            nc.sync.dma_start(out=wgt_sb[:, cols], in_=wgt[:, cols])
+        def load_wgt():
+            nc.sync.dma_start(out=wgt_rows[:], in_=wgt.rearrange("(h m) (c j) -> m h c j", m=RUN, j=P)[0])
+
+        def spread_wgt():
+            first = p_pool.tile([P, P], F32, name="p_bank")
+            nc.tensor.transpose(first[:], wgt_rows[:], ident[:])
+            by_chunk = first[:].rearrange("j (h c) -> j c h", c=S // P)
+            for half in range(2):
+                chunks = slice(half * PACK, (half + 1) * PACK)
+                nc.scalar.copy(
+                    out=wgt_turned[:, chunks, :].rearrange("j c (h m) -> j c h m", m=RUN),
+                    in_=by_chunk[:, chunks, :].unsqueeze(3).to_broadcast([P, PACK, P // RUN, RUN]),
+                )
+            for half in range(2):
+                bank = e_pool.tile([P, PACK, P], F32, name="e_bank")
+                for c in range(PACK):
+                    nc.tensor.transpose(bank[:, c, :], wgt_turned[:, half * PACK + c, :], ident[:])
+                nc.scalar.copy(
+                    out=wgt_sb[:, half * PASS : (half + 1) * PASS], in_=bank[:].rearrange("p c j -> p (c j)")
+                )
 
         def load_x(i):
             nc.sync.dma_start(out=x_plane[i][:], in_=x_rows[i])
@@ -109,25 +130,24 @@ def tile_list_mesh_plastic_force_kernel(
             )
 
         def load_we_scales():
-            for quad in range(QUADS):
+            for r in range(QUADS):
                 nc.sync.dma_start(
-                    out=we_s_raw[32 * quad : 32 * quad + 4, :, :],
-                    in_=we_scales[:, 4 * quad : 4 * quad + 4, :].rearrange("a r n -> r a n").bitcast(I32),
+                    out=we_s_raw[r:P:32, :, :],
+                    in_=we_scales[:, r:16:4, :].rearrange("a q n -> q a n").bitcast(I32),
                 )
 
         def move_scales(a):
-            for quad in range(QUADS):
-                row = 16 * a + 4 * quad
+            for r in range(QUADS):
                 nc.sync.dma_start(
-                    out=v_scales[a][32 * quad : 32 * quad + 4, :].bitcast(I32),
-                    in_=picked_s[row : row + 4, :].bitcast(I32),
+                    out=v_scales[a][r:P:32, :].bitcast(I32),
+                    in_=picked_s[16 * a + r : 16 * (a + 1) : 4, :].bitcast(I32),
                 )
 
         def quantize(codes, scales, values):
             nc.vector.quantize_mx(out=codes.bitcast(FP8X4), scales=scales, in_=values)
 
         def weave(dst, src):
-            nc.scalar.activation(out=dst, in_=src, func=ACT.Copy)
+            nc.scalar.copy(out=dst, in_=src)
 
         def gather_x(i, lo, hi):
             nc.vector.tensor_tensor(
@@ -147,8 +167,10 @@ def tile_list_mesh_plastic_force_kernel(
         def prepare_wp(g):
             for t in range(PACK):
                 weave(
-                    wp_bf[g][:, t * PASS : (t + 1) * PASS].rearrange("p (b i j) -> p b j i", i=RUN, j=PACK),
-                    wp_raw[g][:].rearrange("p j (b t i) -> p t b j i", t=PACK, i=RUN)[:, t],
+                    wp_bf[g][:, t * PASS : (t + 1) * PASS].rearrange(
+                        "p (b c i j) -> p b c j i", c=RUN // LINE, i=LINE, j=PACK
+                    ),
+                    wp_raw[g][:].rearrange("p j (b t c i) -> p t b c j i", t=PACK, c=RUN // LINE, i=LINE)[:, t],
                 )
             quantize(wp_codes[g][:], wp_sc[g][:], wp_bf[g][:])
 
@@ -271,6 +293,8 @@ def tile_list_mesh_plastic_force_kernel(
         for a in range(C_PASSES):
             nc.vector.memset(v_scales[a][:].bitcast(I32), 0)
 
+        load_wgt()
+        make_identity(nc, ident[:])
         nc.sync.dma_start(
             out=tab_s[0:32, :].bitcast(I32), in_=tab_scales.rearrange("a q t -> (a q) t").bitcast(I32)
         )
@@ -278,9 +302,8 @@ def tile_list_mesh_plastic_force_kernel(
         nc.vector.tensor_copy(picked_s[:], tab_s[:].indirect(tab_list[:]))
         nc.sync.dma_start(out=edge_list[:], in_=offs2)
 
-        load_wgt(0)
         load_x(0)
-        load_wgt(1)
+        spread_wgt()
         load_x(1)
         load_x(2)
         load_wp(0)

@@ -31,7 +31,7 @@ QUARTERS = 4
 QW = S // QUARTERS
 CHUNKS = QW // P
 LIST_COLS = QW // 16
-P_BANKS, E_BANKS, Y_BANKS = 2, 3, N_SLICES
+BANKS, E_BANKS = 8, 4
 WF_SPLIT = 512
 
 
@@ -41,9 +41,13 @@ def tile_list_mesh_plastic_force_kernel(
     nc = tc.nc
     with ExitStack() as ctx:
         keep = ctx.enter_context(tc.tile_pool(name="keep", bufs=1))
-        p_pool = ctx.enter_context(tc.psum_pool(name="p_psum", bufs=P_BANKS))
-        e_pool = ctx.enter_context(tc.psum_pool(name="e_psum", bufs=E_BANKS))
-        y_pool = ctx.enter_context(tc.psum_pool(name="y_psum", bufs=Y_BANKS))
+        psum = ctx.enter_context(tc.psum_pool(name="psum", bufs=1))
+        banks = [psum.tile([P, PASS], F32, name="bank%d" % b) for b in range(BANKS)]
+        first_ring, e_ring, py_ring = list(banks), banks[:E_BANKS], banks[E_BANKS:]
+
+        def take(ring):
+            ring.append(ring.pop(0))
+            return ring[-1]
 
         def tile(name, shape, dtype):
             return keep.tile(shape, dtype, name=name, tag=name, align_bytes=64)
@@ -90,9 +94,9 @@ def tile_list_mesh_plastic_force_kernel(
             nc.sync.dma_start(out=wgt_rows[:], in_=wgt.rearrange("(h m) (c j) -> m h c j", m=RUN, j=P)[0])
 
         def spread_wgt():
-            first = p_pool.tile([P, P], F32, name="p_bank")
-            nc.tensor.transpose(first[:], wgt_rows[:], ident[:])
-            by_chunk = first[:].rearrange("j (h c) -> j c h", c=S // P)
+            first = banks[0][:, 0:P]
+            nc.tensor.transpose(first, wgt_rows[:], ident[:])
+            by_chunk = first.rearrange("j (h c) -> j c h", c=S // P)
             for half in range(2):
                 chunks = slice(half * PACK, (half + 1) * PACK)
                 nc.scalar.copy(
@@ -100,12 +104,10 @@ def tile_list_mesh_plastic_force_kernel(
                     in_=by_chunk[:, chunks, :].unsqueeze(3).to_broadcast([P, PACK, P // RUN, RUN]),
                 )
             for half in range(2):
-                bank = e_pool.tile([P, PACK, P], F32, name="e_bank")
+                bank = banks[1 + half]
                 for c in range(PACK):
-                    nc.tensor.transpose(bank[:, c, :], wgt_turned[:, half * PACK + c, :], ident[:])
-                nc.scalar.copy(
-                    out=wgt_sb[:, half * PASS : (half + 1) * PASS], in_=bank[:].rearrange("p c j -> p (c j)")
-                )
+                    nc.tensor.transpose(bank[:, c * P : (c + 1) * P], wgt_turned[:, half * PACK + c, :], ident[:])
+                nc.scalar.copy(out=wgt_sb[:, half * PASS : (half + 1) * PASS], in_=bank[:])
 
         def load_x(i):
             nc.sync.dma_start(out=x_plane[i][:], in_=x_rows[i])
@@ -174,14 +176,15 @@ def tile_list_mesh_plastic_force_kernel(
                 )
             quantize(wp_codes[g][:], wp_sc[g][:], wp_bf[g][:])
 
-        def prepare_wf():
-            for g in range(H_PASSES):
-                for s in range(N_SLICES):
-                    lo = (g * N + s * P) * PACK
-                    weave(
-                        wf_bf[:, lo : lo + P * PACK].rearrange("p (c i t) -> p c t i", i=LINE, t=PACK),
-                        wf_raw[g][:, :, s * P : (s + 1) * P].rearrange("p t (c i) -> p c t i", i=LINE),
-                    )
+        def weave_wf(g):
+            for s in range(N_SLICES):
+                lo = (g * N + s * P) * PACK
+                weave(
+                    wf_bf[:, lo : lo + P * PACK].rearrange("p (c i t) -> p c t i", i=LINE, t=PACK),
+                    wf_raw[g][:, :, s * P : (s + 1) * P].rearrange("p t (c i) -> p c t i", i=LINE),
+                )
+
+        def quantize_wf():
             for lo, hi in ((0, WF_SPLIT), (WF_SPLIT, H_PASSES * N)):
                 quantize(wf_codes[:, lo:hi], wf_sc[:, lo:hi], wf_bf[:, lo * PACK : hi * PACK])
 
@@ -204,29 +207,28 @@ def tile_list_mesh_plastic_force_kernel(
 
         def square(u):
             q, g = u
-            for c in range(CHUNKS):
-                bank = p_pool.tile([P, PACK, P], F32, name="p_bank")
-                cols = slice(c * P, (c + 1) * P)
-                for t in range(PACK):
-                    w = slice(t * P, (t + 1) * P)
+            for u2 in range(PACK // 2):
+                bank = take(first_ring if g == 0 else py_ring)[:].rearrange("p (t n) -> p t n", t=2)
+                for t2 in range(2):
+                    w = slice((2 * u2 + t2) * P, (2 * u2 + t2 + 1) * P)
                     nc.tensor.matmul_mx(
-                        out=bank[:, t, :],
+                        out=bank[:, t2, :],
                         lhsT=wp_codes[g][:, w].bitcast(FP8X4),
                         lhsT_scale=wp_sc[g][:, w],
-                        rhs=xg_codes[q][:, cols].bitcast(FP8X4),
-                        rhs_scale=xg_sc[q][:, cols],
+                        rhs=xg_codes[q][:].bitcast(FP8X4),
+                        rhs_scale=xg_sc[q][:],
                         start=True,
                         stop=True,
                     )
                 nc.scalar.activation(
-                    out=sq[u][:, c * PASS : (c + 1) * PASS].rearrange("p (n t i) -> p n t i", t=PACK, i=PAIR),
+                    out=sq[u][:].rearrange("p (n t i) -> p n t i", t=PACK, i=PAIR)[:, :, 2 * u2 : 2 * u2 + 2, :],
                     in_=bank[:].rearrange("p t (n i) -> p n t i", i=PAIR),
                     func=ACT.Square,
                 )
 
         def subtract(u, c):
             q, g = u
-            bank = e_pool.tile([P, PACK, P], F32, name="e_bank")
+            bank = take(e_ring)[:].rearrange("p (t n) -> p t n", t=PACK)
             cols = slice(q * QW + c * P, q * QW + (c + 1) * P)
             for t in range(PACK):
                 for a in range(C_PASSES):
@@ -255,10 +257,7 @@ def tile_list_mesh_plastic_force_kernel(
         def force(q, lo, hi):
             last = q == QUARTERS - 1 and hi == QW
             for s in range(N_SLICES):
-                if last and s < P_BANKS:
-                    bank = p_pool.tile([P, hi - lo], F32, name="p_bank")
-                else:
-                    bank = y_pool.tile([P, hi - lo], F32, name="y_bank")
+                bank = take(e_ring if last else py_ring)[:, 0 : hi - lo]
                 for g in range(H_PASSES):
                     w = slice(g * N + s * P, g * N + (s + 1) * P)
                     nc.tensor.matmul_mx(
@@ -326,27 +325,30 @@ def tile_list_mesh_plastic_force_kernel(
         for i in range(1, PACK - 1):
             gather_x(i, 0, QUARTERS)
         prepare_wp(0)
-        for q in range(QUARTERS):
+        x_order = [0, 1, 2, 3]
+        for q in x_order:
             gather_x(PACK - 1, q, q + 1)
-        for q in range(QUARTERS):
+        for q in x_order:
             prepare_x(q)
+        for q in x_order:
+            if q == 3:
+                prepare_wp(1)
             square((q, 0))
         gather_tab(0, 0, 2)
         order_we(0)
-        gather_tab(1, 0, 1)
         gather_tab(0, 2, QUARTERS)
-        prepare_wp(1)
+        gather_tab(1, 0, 1)
+        gather_tab(1, 1, QUARTERS)
+        order_we(1)
+        square((0, 1))
+        square((1, 1))
+        weave_wf(0)
+        weave_wf(1)
+        quantize_wf()
+        square((2, 1))
+        square((3, 1))
 
         for n, u in enumerate(units):
-            q, g = u
-            if g == 0 and q + 1 < QUARTERS:
-                gather_tab(1, q + 1, q + 2)
-            if n == 1:
-                order_we(1)
-            if QUARTERS <= n + 1 < len(units):
-                square(units[n + 1])
-            if u == (0, 1):
-                prepare_wf()
             subtract(u, 0)
             if n > 0:
                 clamp(units[n - 1], 0, QW)

@@ -97,17 +97,16 @@ def tile_list_mesh_plastic_force_kernel(
             first = banks[0][:, 0:P]
             nc.tensor.transpose(first, wgt_rows[:], ident[:])
             by_chunk = first.rearrange("j (h c) -> j c h", c=S // P)
-            for half in range(2):
-                chunks = slice(half * PACK, (half + 1) * PACK)
+            for q in range(QUARTERS):
+                chunks = slice(q * CHUNKS, (q + 1) * CHUNKS)
                 nc.scalar.copy(
                     out=wgt_turned[:, chunks, :].rearrange("j c (h m) -> j c h m", m=RUN),
-                    in_=by_chunk[:, chunks, :].unsqueeze(3).to_broadcast([P, PACK, P // RUN, RUN]),
+                    in_=by_chunk[:, chunks, :].unsqueeze(3).to_broadcast([P, CHUNKS, P // RUN, RUN]),
                 )
-            for half in range(2):
-                bank = banks[1 + half]
-                for c in range(PACK):
-                    nc.tensor.transpose(bank[:, c * P : (c + 1) * P], wgt_turned[:, half * PACK + c, :], ident[:])
-                nc.scalar.copy(out=wgt_sb[:, half * PASS : (half + 1) * PASS], in_=bank[:])
+                bank = banks[1 + q]
+                for c in range(CHUNKS):
+                    nc.tensor.transpose(bank[:, c * P : (c + 1) * P], wgt_turned[:, q * CHUNKS + c, :], ident[:])
+                nc.scalar.copy(out=wgt_sb[:, q * QW : (q + 1) * QW], in_=bank[:, 0:QW])
 
         def load_x(i):
             nc.sync.dma_start(out=x_plane[i][:], in_=x_rows[i])
@@ -305,8 +304,8 @@ def tile_list_mesh_plastic_force_kernel(
         spread_wgt()
         load_x(1)
         load_x(2)
-        load_wp(0)
         load_x(3)
+        load_wp(0)
         load_we_scales()
         load_tab(0)
         load_we(0)
@@ -320,15 +319,17 @@ def tile_list_mesh_plastic_force_kernel(
         with nc.allow_non_contiguous_dma(reason="one bias value a partition"):
             nc.sync.dma_start(out=bias[:], in_=load.rearrange("(s p) -> p s", p=P))
 
-        for half in range(2):
-            gather_x(0, 2 * half, 2 * half + 2)
+        gather_x(0, 0, 1)
+        gather_x(0, 1, 2)
+        gather_x(0, 2, QUARTERS)
         for i in range(1, PACK - 1):
             gather_x(i, 0, QUARTERS)
-        prepare_wp(0)
         x_order = [0, 1, 2, 3]
         for q in x_order:
             gather_x(PACK - 1, q, q + 1)
         for q in x_order:
+            if q == 2:
+                prepare_wp(0)
             prepare_x(q)
         for q in x_order:
             if q == 3:

@@ -32,6 +32,7 @@ QW = S // QUARTERS
 CHUNKS = QW // P
 LIST_COLS = QW // 16
 BANKS, E_BANKS = 8, 4
+VECTOR_SLICES = 2
 WF_SPLIT = 512
 
 
@@ -66,8 +67,6 @@ def tile_list_mesh_plastic_force_kernel(
         v_scales = [tile("v_scales%d" % a, [P, S], U8) for a in range(C_PASSES)]
         we_raw = [tile("we_raw%d" % g, [P, C_PASSES, PASS // 2], I32) for g in range(H_PASSES)]
         we_s_raw = tile("we_s_raw", [P, C_PASSES, H // 4], I32)
-        we_codes = [tile("we_codes%d" % g, [P, C_PASSES * PASS * 2], U8) for g in range(H_PASSES)]
-        we_sc = [tile("we_sc%d" % g, [P, C_PASSES * PASS], U8) for g in range(H_PASSES)]
         wp_bf = [tile("wp_bf%d" % g, [P, PASS * PACK], BF16) for g in range(H_PASSES)]
         wp_codes = [tile("wp_codes%d" % g, [P, PASS], U32) for g in range(H_PASSES)]
         wp_sc = [tile("wp_sc%d" % g, [P, PASS], U8) for g in range(H_PASSES)]
@@ -76,13 +75,23 @@ def tile_list_mesh_plastic_force_kernel(
         wf_sc = tile("wf_sc", [P, H_PASSES * N], U8)
         xg = tile("xg", [P, PACK, S], F32)
         xg_bf = [tile("xg_bf%d" % q, [P, QW * PACK], BF16) for q in range(QUARTERS)]
+        we_sc = keep.tile([P, C_PASSES * H], U8, name="we_sc", tag="xg_bf2", align_bytes=64)
+        we_codes = [
+            keep.tile([P, C_PASSES * PASS * 2], U8, name="we_codes0", tag="xg_bf3", align_bytes=64),
+            tile("we_codes1", [P, C_PASSES * PASS * 2], U8),
+        ]
         xg_codes = [tile("xg_codes%d" % q, [P, QW], U32) for q in range(QUARTERS)]
         xg_sc = [tile("xg_sc%d" % q, [P, QW], U8) for q in range(QUARTERS)]
         bias = tile("bias", [P, N_SLICES], F32)
         units = [(q, g) for g in range(H_PASSES) for q in range(QUARTERS)]
         sq = {u: tile("sq%d_%d" % u, [P, QW * PACK], F32) for u in units}
-        h_bf = {u: tile("h_bf%d_%d" % u, [P, QW * PACK], BF16) for u in units}
-        h_codes = {u: tile("h_codes%d_%d" % u, [P, QW], U32) for u in units}
+        held = [(2, 0), (3, 0)]
+        h_bf = {u: tile("h_bf%d_%d" % u, [P, QW * PACK], BF16)[:] for u in units if u not in held}
+        h_held = keep.tile([P, len(held), QW * PACK], BF16, name="h_held", tag="wp_raw1", align_bytes=64)
+        for n, u in enumerate(held):
+            h_bf[u] = h_held[:, n, :]
+        h_codes = {u: tile("h_codes%d_%d" % u, [P, QW], U32) for u in units if u != (1, 0)}
+        h_codes[(1, 0)] = keep.tile([P, QW], U32, name="h_codes1_0", tag="wf_raw0", align_bytes=64)
         h_sc = {u: tile("h_sc%d_%d" % u, [P, QW], U8) for u in units}
         y_sb = [tile("y_sb%d" % q, [P, N_SLICES, QW], F32) for q in range(QUARTERS)]
         wp_raw = [tile("wp_raw%d" % g, [P, PACK, PASS], F32) for g in range(H_PASSES)]
@@ -167,12 +176,14 @@ def tile_list_mesh_plastic_force_kernel(
 
         def prepare_wp(g):
             for t in range(PACK):
-                weave(
-                    wp_bf[g][:, t * PASS : (t + 1) * PASS].rearrange(
-                        "p (b c i j) -> p b c j i", c=RUN // LINE, i=LINE, j=PACK
-                    ),
-                    wp_raw[g][:].rearrange("p j (b t c i) -> p t b c j i", t=PACK, c=RUN // LINE, i=LINE)[:, t],
+                dst = wp_bf[g][:, t * PASS : (t + 1) * PASS].rearrange(
+                    "p (b c i j) -> p b c j i", c=RUN // LINE, i=LINE, j=PACK
                 )
+                src = wp_raw[g][:].rearrange("p j (b t c i) -> p t b c j i", t=PACK, c=RUN // LINE, i=LINE)[:, t]
+                if g == 0 and t >= PACK - VECTOR_SLICES:
+                    nc.vector.tensor_copy(out=dst, in_=src)
+                else:
+                    weave(dst, src)
             quantize(wp_codes[g][:], wp_sc[g][:], wp_bf[g][:])
 
         def weave_wf(g):
@@ -188,14 +199,15 @@ def tile_list_mesh_plastic_force_kernel(
                 quantize(wf_codes[:, lo:hi], wf_sc[:, lo:hi], wf_bf[:, lo * PACK : hi * PACK])
 
         def order_we(g):
-            nc.vector.tensor_copy(
+            nc.gpsimd.tensor_copy(
                 out=we_codes[g][:].bitcast(I32).rearrange("p (a t b w) -> p a t b w", a=C_PASSES, t=PACK, w=4),
                 in_=we_raw[g][:].rearrange("p a (b t w) -> p a t b w", t=PACK, w=4),
             )
-            words = PASS // 4
-            nc.vector.tensor_copy(
-                out=we_sc[g][:].bitcast(I32).rearrange("p (a t b w) -> p a t b w", a=C_PASSES, t=PACK, w=2),
-                in_=we_s_raw[:, :, g * words : (g + 1) * words].rearrange("p a (b t w) -> p a t b w", t=PACK, w=2),
+
+        def order_we_scales():
+            nc.gpsimd.tensor_copy(
+                out=we_sc[:].bitcast(I32).rearrange("p (u t b w) -> p u t b w", u=C_PASSES * H_PASSES, t=PACK, w=2),
+                in_=we_s_raw[:].rearrange("p a (g b t w) -> p (a g) t b w", g=H_PASSES, t=PACK, w=2),
             )
 
         def gather_tab(a, lo, hi):
@@ -235,7 +247,7 @@ def tile_list_mesh_plastic_force_kernel(
                     nc.tensor.matmul_mx(
                         out=bank[:, t, :],
                         lhsT=we_codes[g][:, 2 * lo : 2 * (lo + P)].bitcast(FP4X4),
-                        lhsT_scale=we_sc[g][:, lo : lo + P],
+                        lhsT_scale=we_sc[:, a * H + g * PASS + t * P : a * H + g * PASS + (t + 1) * P],
                         rhs=v_codes[a][:, cols].bitcast(FP8X4),
                         rhs_scale=v_scales[a][:, cols],
                         start=(a == 0),
@@ -306,11 +318,11 @@ def tile_list_mesh_plastic_force_kernel(
         load_x(2)
         load_x(3)
         load_wp(0)
-        load_we_scales()
         load_tab(0)
-        load_we(0)
-        move_scales(0)
+        load_we_scales()
         load_tab(1)
+        move_scales(0)
+        load_we(0)
         move_scales(1)
         load_wp(1)
         load_we(1)
@@ -325,10 +337,11 @@ def tile_list_mesh_plastic_force_kernel(
         for i in range(1, PACK - 1):
             gather_x(i, 0, QUARTERS)
         x_order = [0, 1, 2, 3]
+        gather_x(PACK - 1, 0, 1)
+        gather_x(PACK - 1, 1, 2)
+        gather_x(PACK - 1, 2, QUARTERS)
         for q in x_order:
-            gather_x(PACK - 1, q, q + 1)
-        for q in x_order:
-            if q == 2:
+            if q == 1:
                 prepare_wp(0)
             prepare_x(q)
         for q in x_order:
@@ -336,6 +349,7 @@ def tile_list_mesh_plastic_force_kernel(
                 prepare_wp(1)
             square((q, 0))
         gather_tab(0, 0, 2)
+        order_we_scales()
         order_we(0)
         gather_tab(0, 2, QUARTERS)
         gather_tab(1, 0, 1)

@@ -67,6 +67,7 @@ def tile_list_mesh_plastic_force_kernel(
         v_scales = [tile("v_scales%d" % a, [P, S], U8) for a in range(C_PASSES)]
         we_raw = [tile("we_raw%d" % g, [P, C_PASSES, PASS // 2], I32) for g in range(H_PASSES)]
         we_s_raw = tile("we_s_raw", [P, C_PASSES, H // 4], I32)
+        we_codes = [tile("we_codes%d" % g, [P, C_PASSES * PASS * 2], U8) for g in range(H_PASSES)]
         wp_bf = [tile("wp_bf%d" % g, [P, PASS * PACK], BF16) for g in range(H_PASSES)]
         wp_codes = [tile("wp_codes%d" % g, [P, PASS], U32) for g in range(H_PASSES)]
         wp_sc = [tile("wp_sc%d" % g, [P, PASS], U8) for g in range(H_PASSES)]
@@ -75,10 +76,9 @@ def tile_list_mesh_plastic_force_kernel(
         wf_sc = tile("wf_sc", [P, H_PASSES * N], U8)
         xg = tile("xg", [P, PACK, S], F32)
         xg_bf = [tile("xg_bf%d" % q, [P, QW * PACK], BF16) for q in range(QUARTERS)]
-        we_sc = keep.tile([P, C_PASSES * H], U8, name="we_sc", tag="xg_bf2", align_bytes=64)
-        we_codes = [
-            keep.tile([P, C_PASSES * PASS * 2], U8, name="we_codes0", tag="xg_bf3", align_bytes=64),
-            tile("we_codes1", [P, C_PASSES * PASS * 2], U8),
+        we_sc = [
+            tile("we_sc0", [P, C_PASSES * PASS], U8),
+            keep.tile([P, C_PASSES * PASS], U8, name="we_sc1", tag="xg_bf%d" % (QUARTERS - 1), align_bytes=64),
         ]
         xg_codes = [tile("xg_codes%d" % q, [P, QW], U32) for q in range(QUARTERS)]
         xg_sc = [tile("xg_sc%d" % q, [P, QW], U8) for q in range(QUARTERS)]
@@ -199,15 +199,15 @@ def tile_list_mesh_plastic_force_kernel(
                 quantize(wf_codes[:, lo:hi], wf_sc[:, lo:hi], wf_bf[:, lo * PACK : hi * PACK])
 
         def order_we(g):
-            nc.gpsimd.tensor_copy(
+            mover = (nc.vector, nc.gpsimd)[g]
+            mover.tensor_copy(
                 out=we_codes[g][:].bitcast(I32).rearrange("p (a t b w) -> p a t b w", a=C_PASSES, t=PACK, w=4),
                 in_=we_raw[g][:].rearrange("p a (b t w) -> p a t b w", t=PACK, w=4),
             )
-
-        def order_we_scales():
-            nc.gpsimd.tensor_copy(
-                out=we_sc[:].bitcast(I32).rearrange("p (u t b w) -> p u t b w", u=C_PASSES * H_PASSES, t=PACK, w=2),
-                in_=we_s_raw[:].rearrange("p a (g b t w) -> p (a g) t b w", g=H_PASSES, t=PACK, w=2),
+            words = PASS // 4
+            mover.tensor_copy(
+                out=we_sc[g][:].bitcast(I32).rearrange("p (a t b w) -> p a t b w", a=C_PASSES, t=PACK, w=2),
+                in_=we_s_raw[:, :, g * words : (g + 1) * words].rearrange("p a (b t w) -> p a t b w", t=PACK, w=2),
             )
 
         def gather_tab(a, lo, hi):
@@ -247,7 +247,7 @@ def tile_list_mesh_plastic_force_kernel(
                     nc.tensor.matmul_mx(
                         out=bank[:, t, :],
                         lhsT=we_codes[g][:, 2 * lo : 2 * (lo + P)].bitcast(FP4X4),
-                        lhsT_scale=we_sc[:, a * H + g * PASS + t * P : a * H + g * PASS + (t + 1) * P],
+                        lhsT_scale=we_sc[g][:, lo : lo + P],
                         rhs=v_codes[a][:, cols].bitcast(FP8X4),
                         rhs_scale=v_scales[a][:, cols],
                         start=(a == 0),
@@ -319,13 +319,13 @@ def tile_list_mesh_plastic_force_kernel(
         load_x(3)
         load_wp(0)
         load_tab(0)
+        load_we(0)
         load_we_scales()
         load_tab(1)
         move_scales(0)
-        load_we(0)
+        load_we(1)
         move_scales(1)
         load_wp(1)
-        load_we(1)
         for g in range(H_PASSES):
             load_wf(g)
         with nc.allow_non_contiguous_dma(reason="one bias value a partition"):
@@ -349,7 +349,6 @@ def tile_list_mesh_plastic_force_kernel(
                 prepare_wp(1)
             square((q, 0))
         gather_tab(0, 0, 2)
-        order_we_scales()
         order_we(0)
         gather_tab(0, 2, QUARTERS)
         gather_tab(1, 0, 1)

@@ -187,11 +187,13 @@ def tile_list_mesh_plastic_force_kernel(
             quantize(wp_codes[g][:], wp_sc[g][:], wp_bf[g][:])
 
         def weave_wf(g):
-            for s in range(N_SLICES):
-                lo = (g * N + s * P) * PACK
+            for half in range(2):
+                lo, hi = half * N // 2, (half + 1) * N // 2
                 weave(
-                    wf_bf[:, lo : lo + P * PACK].rearrange("p (c i t) -> p c t i", i=LINE, t=PACK),
-                    wf_raw[g][:, :, s * P : (s + 1) * P].rearrange("p t (c i) -> p c t i", i=LINE),
+                    wf_bf[:, (g * N + lo) * PACK : (g * N + hi) * PACK].rearrange(
+                        "p (c i t) -> p c t i", i=LINE, t=PACK
+                    ),
+                    wf_raw[g][:, :, lo:hi].rearrange("p t (c i) -> p c t i", i=LINE),
                 )
 
         def quantize_wf():
@@ -232,9 +234,7 @@ def tile_list_mesh_plastic_force_kernel(
                         stop=True,
                     )
                 nc.scalar.activation(
-                    out=sq[u][:].rearrange("p (n t i) -> p n t i", t=PACK, i=PAIR)[:, :, 2 * u2 : 2 * u2 + 2, :],
-                    in_=bank[:].rearrange("p t (n i) -> p n t i", i=PAIR),
-                    func=ACT.Square,
+                    out=sq[u][:, u2 * PASS : (u2 + 1) * PASS], in_=bank.rearrange("p t n -> p (t n)"), func=ACT.Square
                 )
 
         def subtract(u, c):
@@ -256,7 +256,7 @@ def tile_list_mesh_plastic_force_kernel(
             part = slice(c * PASS, (c + 1) * PASS)
             nc.vector.tensor_tensor(
                 h_bf[u][:, part].rearrange("p (n i t) -> p n t i", t=PACK, i=PAIR),
-                sq[u][:, part].rearrange("p (n t i) -> p n t i", t=PACK, i=PAIR),
+                sq[u][:].rearrange("p (t c n i) -> p c n t i", t=PACK, c=CHUNKS, i=PAIR)[:, c],
                 bank[:].rearrange("p t (n i) -> p n t i", i=PAIR),
                 ALU.subtract,
             )
@@ -268,7 +268,13 @@ def tile_list_mesh_plastic_force_kernel(
         def force(q, lo, hi):
             last = q == QUARTERS - 1 and hi == QW
             for s in range(N_SLICES):
-                bank = take(e_ring if last else py_ring)[:, 0 : hi - lo]
+                if q == QUARTERS - 2 and s > 0:
+                    bank = banks[s - 1]
+                elif last and s < 2:
+                    bank = banks[s + 2]
+                else:
+                    bank = take(py_ring)
+                bank = bank[:, 0 : hi - lo]
                 for g in range(H_PASSES):
                     w = slice(g * N + s * P, g * N + (s + 1) * P)
                     nc.tensor.matmul_mx(
@@ -280,7 +286,7 @@ def tile_list_mesh_plastic_force_kernel(
                         start=(g == 0),
                         stop=(g == H_PASSES - 1),
                     )
-                if last and s % 2 == 0:
+                if q == QUARTERS - 1 and s % 2 == 0:
                     nc.vector.tensor_scalar_add(y_sb[q][:, s, lo:hi], bank[:], bias[:, s : s + 1])
                 else:
                     nc.scalar.activation(
@@ -297,19 +303,19 @@ def tile_list_mesh_plastic_force_kernel(
             if g == H_PASSES - 1:
                 force(q, lo, hi)
 
-        nc.vector.memset(we_s_raw[:], 0)
         nc.vector.memset(tab_s[32:64, :].bitcast(I32), 0)
         nc.vector.memset(tab_s[64:128, :].bitcast(I32), 0)
+        nc.vector.memset(we_s_raw[:], 0)
         for a in range(C_PASSES):
             nc.vector.memset(v_scales[a][:].bitcast(I32), 0)
 
-        load_wgt()
         make_identity(nc, ident[:])
         nc.sync.dma_start(
             out=tab_s[0:32, :].bitcast(I32), in_=tab_scales.rearrange("a q t -> (a q) t").bitcast(I32)
         )
         nc.sync.dma_start(out=tab_list[:], in_=offs)
         nc.vector.tensor_copy(picked_s[:], tab_s[:].indirect(tab_list[:]))
+        load_wgt()
         nc.sync.dma_start(out=edge_list[:], in_=offs2)
 
         load_x(0)

@@ -67,7 +67,6 @@ def tile_list_mesh_plastic_force_kernel(
         v_scales = [tile("v_scales%d" % a, [P, S], U8) for a in range(C_PASSES)]
         we_raw = [tile("we_raw%d" % g, [P, C_PASSES, PASS // 2], I32) for g in range(H_PASSES)]
         we_s_raw = tile("we_s_raw", [P, C_PASSES, H // 4], I32)
-        we_codes = [tile("we_codes%d" % g, [P, C_PASSES * PASS * 2], U8) for g in range(H_PASSES)]
         wp_bf = [tile("wp_bf%d" % g, [P, PASS * PACK], BF16) for g in range(H_PASSES)]
         wp_codes = [tile("wp_codes%d" % g, [P, PASS], U32) for g in range(H_PASSES)]
         wp_sc = [tile("wp_sc%d" % g, [P, PASS], U8) for g in range(H_PASSES)]
@@ -76,9 +75,10 @@ def tile_list_mesh_plastic_force_kernel(
         wf_sc = tile("wf_sc", [P, H_PASSES * N], U8)
         xg = tile("xg", [P, PACK, S], F32)
         xg_bf = [tile("xg_bf%d" % q, [P, QW * PACK], BF16) for q in range(QUARTERS)]
-        we_sc = [
-            tile("we_sc0", [P, C_PASSES * PASS], U8),
-            keep.tile([P, C_PASSES * PASS], U8, name="we_sc1", tag="xg_bf%d" % (QUARTERS - 1), align_bytes=64),
+        we_sc = keep.tile([P, C_PASSES * H], U8, name="we_sc", tag="xg_bf2", align_bytes=64)
+        we_codes = [
+            keep.tile([P, C_PASSES * PASS * 2], U8, name="we_codes0", tag="xg_bf3", align_bytes=64),
+            tile("we_codes1", [P, C_PASSES * PASS * 2], U8),
         ]
         xg_codes = [tile("xg_codes%d" % q, [P, QW], U32) for q in range(QUARTERS)]
         xg_sc = [tile("xg_sc%d" % q, [P, QW], U8) for q in range(QUARTERS)]
@@ -201,15 +201,15 @@ def tile_list_mesh_plastic_force_kernel(
                 quantize(wf_codes[:, lo:hi], wf_sc[:, lo:hi], wf_bf[:, lo * PACK : hi * PACK])
 
         def order_we(g):
-            mover = (nc.vector, nc.gpsimd)[g]
-            mover.tensor_copy(
+            nc.gpsimd.tensor_copy(
                 out=we_codes[g][:].bitcast(I32).rearrange("p (a t b w) -> p a t b w", a=C_PASSES, t=PACK, w=4),
                 in_=we_raw[g][:].rearrange("p a (b t w) -> p a t b w", t=PACK, w=4),
             )
-            words = PASS // 4
-            mover.tensor_copy(
-                out=we_sc[g][:].bitcast(I32).rearrange("p (a t b w) -> p a t b w", a=C_PASSES, t=PACK, w=2),
-                in_=we_s_raw[:, :, g * words : (g + 1) * words].rearrange("p a (b t w) -> p a t b w", t=PACK, w=2),
+
+        def order_we_scales():
+            nc.gpsimd.tensor_copy(
+                out=we_sc[:].bitcast(I32).rearrange("p (u t b w) -> p u t b w", u=C_PASSES * H_PASSES, t=PACK, w=2),
+                in_=we_s_raw[:].rearrange("p a (g b t w) -> p (a g) t b w", g=H_PASSES, t=PACK, w=2),
             )
 
         def gather_tab(a, lo, hi):
@@ -247,7 +247,7 @@ def tile_list_mesh_plastic_force_kernel(
                     nc.tensor.matmul_mx(
                         out=bank[:, t, :],
                         lhsT=we_codes[g][:, 2 * lo : 2 * (lo + P)].bitcast(FP4X4),
-                        lhsT_scale=we_sc[g][:, lo : lo + P],
+                        lhsT_scale=we_sc[:, a * H + g * PASS + t * P : a * H + g * PASS + (t + 1) * P],
                         rhs=v_codes[a][:, cols].bitcast(FP8X4),
                         rhs_scale=v_scales[a][:, cols],
                         start=(a == 0),
@@ -325,12 +325,12 @@ def tile_list_mesh_plastic_force_kernel(
         load_x(3)
         load_wp(0)
         load_tab(0)
+        move_scales(0)
         load_we(0)
         load_we_scales()
         load_tab(1)
-        move_scales(0)
-        load_we(1)
         move_scales(1)
+        load_we(1)
         load_wp(1)
         for g in range(H_PASSES):
             load_wf(g)
@@ -355,6 +355,7 @@ def tile_list_mesh_plastic_force_kernel(
                 prepare_wp(1)
             square((q, 0))
         gather_tab(0, 0, 2)
+        order_we_scales()
         order_we(0)
         gather_tab(0, 2, QUARTERS)
         gather_tab(1, 0, 1)

@@ -75,7 +75,10 @@ def tile_list_mesh_plastic_force_kernel(
         wf_sc = tile("wf_sc", [P, H_PASSES * N], U8)
         xg = tile("xg", [P, PACK, S], F32)
         xg_bf = [tile("xg_bf%d" % q, [P, QW * PACK], BF16) for q in range(QUARTERS)]
-        we_sc = keep.tile([P, C_PASSES * H], U8, name="we_sc", tag="xg_bf2", align_bytes=64)
+        we_sc = [
+            tile("we_sc0", [P, C_PASSES * PASS], U8),
+            keep.tile([P, C_PASSES * PASS], U8, name="we_sc1", tag="we_raw0", align_bytes=64),
+        ]
         we_codes = [
             keep.tile([P, C_PASSES * PASS * 2], U8, name="we_codes0", tag="xg_bf3", align_bytes=64),
             tile("we_codes1", [P, C_PASSES * PASS * 2], U8),
@@ -206,10 +209,11 @@ def tile_list_mesh_plastic_force_kernel(
                 in_=we_raw[g][:].rearrange("p a (b t w) -> p a t b w", t=PACK, w=4),
             )
 
-        def order_we_scales():
-            nc.gpsimd.tensor_copy(
-                out=we_sc[:].bitcast(I32).rearrange("p (u t b w) -> p u t b w", u=C_PASSES * H_PASSES, t=PACK, w=2),
-                in_=we_s_raw[:].rearrange("p a (g b t w) -> p (a g) t b w", g=H_PASSES, t=PACK, w=2),
+        def order_we_scales(g):
+            words = PASS // 4
+            (nc.vector, nc.gpsimd)[g].tensor_copy(
+                out=we_sc[g][:].bitcast(I32).rearrange("p (a t b w) -> p a t b w", a=C_PASSES, t=PACK, w=2),
+                in_=we_s_raw[:, :, g * words : (g + 1) * words].rearrange("p a (b t w) -> p a t b w", t=PACK, w=2),
             )
 
         def gather_tab(a, lo, hi):
@@ -247,7 +251,7 @@ def tile_list_mesh_plastic_force_kernel(
                     nc.tensor.matmul_mx(
                         out=bank[:, t, :],
                         lhsT=we_codes[g][:, 2 * lo : 2 * (lo + P)].bitcast(FP4X4),
-                        lhsT_scale=we_sc[:, a * H + g * PASS + t * P : a * H + g * PASS + (t + 1) * P],
+                        lhsT_scale=we_sc[g][:, lo : lo + P],
                         rhs=v_codes[a][:, cols].bitcast(FP8X4),
                         rhs_scale=v_scales[a][:, cols],
                         start=(a == 0),
@@ -355,8 +359,9 @@ def tile_list_mesh_plastic_force_kernel(
                 prepare_wp(1)
             square((q, 0))
         gather_tab(0, 0, 2)
-        order_we_scales()
+        order_we_scales(0)
         order_we(0)
+        order_we_scales(1)
         gather_tab(0, 2, QUARTERS)
         gather_tab(1, 0, 1)
         gather_tab(1, 1, QUARTERS)

@@ -123,8 +123,9 @@ def tile_list_mesh_plastic_force_kernel(
         def load_x(i):
             nc.sync.dma_start(out=x_plane[i][:], in_=x_rows[i])
 
-        def load_tab(a):
-            nc.sync.dma_start(out=tab_w[a][:], in_=tab_words[a].rearrange("p t i -> p (t i)").bitcast(I32))
+        def load_tab(a, lo=0, hi=T):
+            words = tab_words[a].rearrange("p t i -> p (t i)").bitcast(I32)
+            nc.sync.dma_start(out=tab_w[a][:, lo:hi], in_=words[:, lo:hi])
 
         def load_wp(g):
             nc.sync.dma_start(
@@ -329,10 +330,11 @@ def tile_list_mesh_plastic_force_kernel(
         load_x(3)
         load_wp(0)
         load_tab(0)
-        move_scales(0)
-        load_we(0)
         load_we_scales()
-        load_tab(1)
+        load_tab(1, 0, T // 2)
+        load_we(0)
+        move_scales(0)
+        load_tab(1, T // 2, T)
         move_scales(1)
         load_we(1)
         load_wp(1)

@@ -123,9 +123,8 @@ def tile_list_mesh_plastic_force_kernel(
         def load_x(i):
             nc.sync.dma_start(out=x_plane[i][:], in_=x_rows[i])
 
-        def load_tab(a, lo=0, hi=T):
-            words = tab_words[a].rearrange("p t i -> p (t i)").bitcast(I32)
-            nc.sync.dma_start(out=tab_w[a][:, lo:hi], in_=words[:, lo:hi])
+        def load_tab(a):
+            nc.sync.dma_start(out=tab_w[a][:], in_=tab_words[a].rearrange("p t i -> p (t i)").bitcast(I32))
 
         def load_wp(g):
             nc.sync.dma_start(
@@ -242,9 +241,12 @@ def tile_list_mesh_plastic_force_kernel(
                     out=sq[u][:, u2 * PASS : (u2 + 1) * PASS], in_=bank.rearrange("p t n -> p (t n)"), func=ACT.Square
                 )
 
+        done = []
+
         def subtract(u, c):
             q, g = u
-            bank = take(e_ring)[:].rearrange("p (t n) -> p t n", t=PACK)
+            whole = take(e_ring)
+            bank = whole[:].rearrange("p (t n) -> p t n", t=PACK)
             cols = slice(q * QW + c * P, q * QW + (c + 1) * P)
             for t in range(PACK):
                 for a in range(C_PASSES):
@@ -265,21 +267,17 @@ def tile_list_mesh_plastic_force_kernel(
                 bank[:].rearrange("p t (n i) -> p n t i", i=PAIR),
                 ALU.subtract,
             )
+            done.append(whole)
+            if len(done) > len(units) * CHUNKS - E_BANKS:
+                py_ring.insert(0, whole)
 
         def clamp(u, lo, hi):
             part = h_bf[u][:, lo * PACK : hi * PACK]
             nc.vector.tensor_scalar_max(part, part, 0.0)
 
         def force(q, lo, hi):
-            last = q == QUARTERS - 1 and hi == QW
             for s in range(N_SLICES):
-                if q == QUARTERS - 2 and s > 0:
-                    bank = banks[s - 1]
-                elif last and s < 2:
-                    bank = banks[s + 2]
-                else:
-                    bank = take(py_ring)
-                bank = bank[:, 0 : hi - lo]
+                bank = take(py_ring)[:, 0 : hi - lo]
                 for g in range(H_PASSES):
                     w = slice(g * N + s * P, g * N + (s + 1) * P)
                     nc.tensor.matmul_mx(
@@ -291,7 +289,7 @@ def tile_list_mesh_plastic_force_kernel(
                         start=(g == 0),
                         stop=(g == H_PASSES - 1),
                     )
-                if q == QUARTERS - 1 and s % 2 == 0:
+                if q == QUARTERS - 1 and hi == QW and s % 2 == 0:
                     nc.vector.tensor_scalar_add(y_sb[q][:, s, lo:hi], bank[:], bias[:, s : s + 1])
                 else:
                     nc.scalar.activation(
@@ -330,11 +328,10 @@ def tile_list_mesh_plastic_force_kernel(
         load_x(3)
         load_wp(0)
         load_tab(0)
-        load_we_scales()
-        load_tab(1, 0, T // 2)
-        load_we(0)
         move_scales(0)
-        load_tab(1, T // 2, T)
+        load_we(0)
+        load_we_scales()
+        load_tab(1)
         move_scales(1)
         load_we(1)
         load_wp(1)
@@ -376,18 +373,18 @@ def tile_list_mesh_plastic_force_kernel(
         square((2, 1))
         square((3, 1))
 
-        for n, u in enumerate(units):
-            subtract(u, 0)
-            if n > 0:
-                clamp(units[n - 1], 0, QW)
-            if n + 1 < len(units):
-                subtract(u, 1)
-                if n > 0:
-                    finish(units[n - 1], 0, QW)
-        u = units[-1]
-        finish(units[-2], 0, QW)
-        clamp(u, 0, P)
-        subtract(u, 1)
-        finish(u, 0, P)
-        clamp(u, P, QW)
-        finish(u, P, QW)
+        steps = [(0, 0, 0, QW), (1, 0, 0, QW), (2, 0, 0, QW), (0, 1, 0, QW), (1, 1, 0, QW), (2, 1, 0, QW), (3, 0, 0, P), (3, 1, 0, P), (3, 0, P, QW), (3, 1, P, QW)]
+        behind = []
+        for q, g, lo, hi in steps:
+            u = (q, g)
+            for c in range(lo // P, hi // P):
+                subtract(u, c)
+                if behind:
+                    step, args = behind.pop(0)
+                    step(*args)
+            behind.extend([(clamp, (u, lo, hi)), (finish, (u, lo, hi))])
+            while len(behind) > 3:
+                step, args = behind.pop(0)
+                step(*args)
+        for step, args in behind:
+            step(*args)

@@ -80,7 +80,7 @@ def tile_list_mesh_plastic_force_kernel(
             keep.tile([P, C_PASSES * PASS], U8, name="we_sc1", tag="we_raw0", align_bytes=64),
         ]
         we_codes = [
-            keep.tile([P, C_PASSES * PASS * 2], U8, name="we_codes0", tag="xg_bf3", align_bytes=64),
+            tile("we_codes0", [P, C_PASSES * PASS * 2], U8),
             tile("we_codes1", [P, C_PASSES * PASS * 2], U8),
         ]
         xg_codes = [tile("xg_codes%d" % q, [P, QW], U32) for q in range(QUARTERS)]
@@ -204,7 +204,7 @@ def tile_list_mesh_plastic_force_kernel(
                 quantize(wf_codes[:, lo:hi], wf_sc[:, lo:hi], wf_bf[:, lo * PACK : hi * PACK])
 
         def order_we(g):
-            nc.gpsimd.tensor_copy(
+            (nc.vector, nc.gpsimd)[g].tensor_copy(
                 out=we_codes[g][:].bitcast(I32).rearrange("p (a t b w) -> p a t b w", a=C_PASSES, t=PACK, w=4),
                 in_=we_raw[g][:].rearrange("p a (b t w) -> p a t b w", t=PACK, w=4),
             )

@@ -248,8 +248,8 @@ def tile_list_mesh_plastic_force_kernel(
             whole = take(e_ring)
             bank = whole[:].rearrange("p (t n) -> p t n", t=PACK)
             cols = slice(q * QW + c * P, q * QW + (c + 1) * P)
-            for t in range(PACK):
-                for a in range(C_PASSES):
+            for a in range(C_PASSES):
+                for t in range(PACK):
                     lo = (a * PACK + t) * P
                     nc.tensor.matmul_mx(
                         out=bank[:, t, :],
@@ -257,8 +257,8 @@ def tile_list_mesh_plastic_force_kernel(
                         lhsT_scale=we_sc[g][:, lo : lo + P],
                         rhs=v_codes[a][:, cols].bitcast(FP8X4),
                         rhs_scale=v_scales[a][:, cols],
-                        start=(a == 0),
-                        stop=(a == C_PASSES - 1),
+                        start=(a == 0 and t == 0),
+                        stop=(a == C_PASSES - 1 and t == PACK - 1),
                     )
             part = slice(c * PASS, (c + 1) * PASS)
             nc.vector.tensor_tensor(
@@ -363,7 +363,8 @@ def tile_list_mesh_plastic_force_kernel(
         order_we_scales(1)
         gather_tab(0, 2, QUARTERS)
         gather_tab(1, 0, 1)
-        gather_tab(1, 1, QUARTERS)
+        gather_tab(1, 1, 2)
+        gather_tab(1, 2, QUARTERS)
         order_we(1)
         square((0, 1))
         square((1, 1))

from contextlib import ExitStack

import concourse.mybir as mybir
from concourse.masks import make_identity

K, C, H, N, T, E, S = 512, 1024, 1024, 384, 2048, 2048, 1024
FLOPS = 2 * S * (K * H + C * H + H * N)

F32 = mybir.dt.float32
BF16 = mybir.dt.bfloat16
I32 = mybir.dt.int32
U32 = mybir.dt.uint32
U16 = mybir.dt.uint16
U8 = mybir.dt.uint8
FP8X4 = mybir.dt.float8_e4m3fn_x4
FP4X4 = mybir.dt.float4_e2m1fn_x4
ALU = mybir.AluOpType
ACT = mybir.ActivationFunctionType

P = 128
PACK = 4
PASS = P * PACK
RUN = 8
LINE = 2
PAIR = 2
QUADS = 4
C_PASSES = C // PASS
H_PASSES = H // PASS
N_SLICES = N // P
QUARTERS = 4
QW = S // QUARTERS
CHUNKS = QW // P
LIST_COLS = QW // 16
BANKS, E_BANKS = 8, 4
VECTOR_SLICES = 2
WF_SPLIT = 512


def tile_list_mesh_plastic_force_kernel(
    tc, xT, wgt, offs2, tab_words, tab_scales, offs, wp, we_words, we_scales, wf, load, out
):
    nc = tc.nc
    with ExitStack() as ctx:
        keep = ctx.enter_context(tc.tile_pool(name="keep", bufs=1))
        psum = ctx.enter_context(tc.psum_pool(name="psum", bufs=1))
        banks = [psum.tile([P, PASS], F32, name="bank%d" % b) for b in range(BANKS)]
        first_ring, e_ring, py_ring = list(banks), banks[:E_BANKS], banks[E_BANKS:]

        def take(ring):
            ring.append(ring.pop(0))
            return ring[-1]

        def tile(name, shape, dtype):
            return keep.tile(shape, dtype, name=name, tag=name, align_bytes=64)

        edge_list = tile("edge_list", [P, S // 16], U16)
        tab_list = tile("tab_list", [P, S // 16], U16)
        wgt_sb = tile("wgt_sb", [P, S], F32)
        wgt_rows = tile("wgt_rows", [P, P], F32)
        wgt_turned = tile("wgt_turned", [P, S // P, P], F32)
        ident = tile("ident", [P, P], F32)
        x_plane = [tile("x_plane%d" % i, [P, E], F32) for i in range(PACK)]
        tab_w = [tile("tab_w%d" % a, [P, T], I32) for a in range(C_PASSES)]
        tab_s = tile("tab_s", [P, T], U8)
        picked_s = tile("picked_s", [P, S], U8)
        v_codes = [tile("v_codes%d" % a, [P, S], U32) for a in range(C_PASSES)]
        v_scales = [tile("v_scales%d" % a, [P, S], U8) for a in range(C_PASSES)]
        we_raw = [tile("we_raw%d" % g, [P, C_PASSES, PASS // 2], I32) for g in range(H_PASSES)]
        we_s_raw = tile("we_s_raw", [P, C_PASSES, H // 4], I32)
        wp_bf = [tile("wp_bf%d" % g, [P, PASS * PACK], BF16) for g in range(H_PASSES)]
        wp_codes = [tile("wp_codes%d" % g, [P, PASS], U32) for g in range(H_PASSES)]
        wp_sc = [tile("wp_sc%d" % g, [P, PASS], U8) for g in range(H_PASSES)]
        wf_bf = tile("wf_bf", [P, H_PASSES * N * PACK], BF16)
        wf_codes = tile("wf_codes", [P, H_PASSES * N], U32)
        wf_sc = tile("wf_sc", [P, H_PASSES * N], U8)
        xg = tile("xg", [P, PACK, S], F32)
        xg_bf = [tile("xg_bf%d" % q, [P, QW * PACK], BF16) for q in range(QUARTERS)]
        we_sc = [
            tile("we_sc0", [P, C_PASSES * PASS], U8),
            keep.tile([P, C_PASSES * PASS], U8, name="we_sc1", tag="we_raw0", align_bytes=64),
        ]
        we_codes = [
            tile("we_codes0", [P, C_PASSES * PASS * 2], U8),
            tile("we_codes1", [P, C_PASSES * PASS * 2], U8),
        ]
        xg_codes = [tile("xg_codes%d" % q, [P, QW], U32) for q in range(QUARTERS)]
        xg_sc = [tile("xg_sc%d" % q, [P, QW], U8) for q in range(QUARTERS)]
        bias = tile("bias", [P, N_SLICES], F32)
        units = [(q, g) for g in range(H_PASSES) for q in range(QUARTERS)]
        sq = {u: tile("sq%d_%d" % u, [P, QW * PACK], F32) for u in units}
        held = [(2, 0), (3, 0)]
        h_bf = {u: tile("h_bf%d_%d" % u, [P, QW * PACK], BF16)[:] for u in units if u not in held}
        h_held = keep.tile([P, len(held), QW * PACK], BF16, name="h_held", tag="wp_raw1", align_bytes=64)
        for n, u in enumerate(held):
            h_bf[u] = h_held[:, n, :]
        h_codes = {u: tile("h_codes%d_%d" % u, [P, QW], U32) for u in units if u != (1, 0)}
        h_codes[(1, 0)] = keep.tile([P, QW], U32, name="h_codes1_0", tag="wf_raw0", align_bytes=64)
        h_sc = {u: tile("h_sc%d_%d" % u, [P, QW], U8) for u in units}
        y_sb = [tile("y_sb%d" % q, [P, N_SLICES, QW], F32) for q in range(QUARTERS)]
        wp_raw = [tile("wp_raw%d" % g, [P, PACK, PASS], F32) for g in range(H_PASSES)]
        wf_raw = [tile("wf_raw%d" % g, [P, PACK, N], F32) for g in range(H_PASSES)]

        x_rows = xT.rearrange("(p i) e -> i p e", i=PACK)

        def load_wgt():
            nc.sync.dma_start(out=wgt_rows[:], in_=wgt.rearrange("(h m) (c j) -> m h c j", m=RUN, j=P)[0])

        def spread_wgt():
            first = banks[0][:, 0:P]
            nc.tensor.transpose(first, wgt_rows[:], ident[:])
            by_chunk = first.rearrange("j (h c) -> j c h", c=S // P)
            for q in range(QUARTERS):
                chunks = slice(q * CHUNKS, (q + 1) * CHUNKS)
                nc.scalar.copy(
                    out=wgt_turned[:, chunks, :].rearrange("j c (h m) -> j c h m", m=RUN),
                    in_=by_chunk[:, chunks, :].unsqueeze(3).to_broadcast([P, CHUNKS, P // RUN, RUN]),
                )
                bank = banks[1 + q]
                for c in range(CHUNKS):
                    nc.tensor.transpose(bank[:, c * P : (c + 1) * P], wgt_turned[:, q * CHUNKS + c, :], ident[:])
                nc.scalar.copy(out=wgt_sb[:, q * QW : (q + 1) * QW], in_=bank[:, 0:QW])

        def load_x(i):
            nc.sync.dma_start(out=x_plane[i][:], in_=x_rows[i])

        def load_tab(a):
            nc.sync.dma_start(out=tab_w[a][:], in_=tab_words[a].rearrange("p t i -> p (t i)").bitcast(I32))

        def load_wp(g):
            nc.sync.dma_start(
                out=wp_raw[g][:], in_=wp[:, g * PASS : (g + 1) * PASS].rearrange("(p j) c -> p j c", j=PACK)
            )

        def load_wf(g):
            rows = wf[g * PASS : (g + 1) * PASS, :].rearrange("(b t i) n -> t b i n", t=PACK, i=RUN)
            for t in range(PACK):
                nc.sync.dma_start(out=wf_raw[g][:, t, :], in_=rows[t])

        def load_we(g):
            nc.sync.dma_start(
                out=we_raw[g][:],
                in_=we_words[:, :, 2 * g * PASS : 2 * (g + 1) * PASS].rearrange("a p n -> p a n").bitcast(I32),
            )

        def load_we_scales():
            for r in range(QUADS):
                nc.sync.dma_start(
                    out=we_s_raw[r:P:32, :, :],
                    in_=we_scales[:, r:16:4, :].rearrange("a q n -> q a n").bitcast(I32),
                )

        def move_scales(a):
            for r in range(QUADS):
                nc.sync.dma_start(
                    out=v_scales[a][r:P:32, :].bitcast(I32),
                    in_=picked_s[16 * a + r : 16 * (a + 1) : 4, :].bitcast(I32),
                )

        def quantize(codes, scales, values):
            nc.vector.quantize_mx(out=codes.bitcast(FP8X4), scales=scales, in_=values)

        def weave(dst, src):
            nc.scalar.copy(out=dst, in_=src)

        def gather_x(i, lo, hi):
            nc.vector.tensor_tensor(
                xg[:, i, lo * QW : hi * QW],
                x_plane[i][:].indirect(edge_list[:, lo * LIST_COLS : hi * LIST_COLS]),
                wgt_sb[:, lo * QW : hi * QW],
                ALU.mult,
            )

        def prepare_x(q):
            weave(
                xg_bf[q][:].rearrange("p (c i t) -> p c t i", i=LINE, t=PACK),
                xg[:, :, q * QW : (q + 1) * QW].rearrange("p t (c i) -> p c t i", i=LINE),
            )
            quantize(xg_codes[q][:], xg_sc[q][:], xg_bf[q][:])

        def prepare_wp(g):
            for t in range(PACK):
                dst = wp_bf[g][:, t * PASS : (t + 1) * PASS].rearrange(
                    "p (b c i j) -> p b c j i", c=RUN // LINE, i=LINE, j=PACK
                )
                src = wp_raw[g][:].rearrange("p j (b t c i) -> p t b c j i", t=PACK, c=RUN // LINE, i=LINE)[:, t]
                if g == 0 and t >= PACK - VECTOR_SLICES:
                    nc.vector.tensor_copy(out=dst, in_=src)
                else:
                    weave(dst, src)
            quantize(wp_codes[g][:], wp_sc[g][:], wp_bf[g][:])

        def weave_wf(g):
            for half in range(2):
                lo, hi = half * N // 2, (half + 1) * N // 2
                weave(
                    wf_bf[:, (g * N + lo) * PACK : (g * N + hi) * PACK].rearrange(
                        "p (c i t) -> p c t i", i=LINE, t=PACK
                    ),
                    wf_raw[g][:, :, lo:hi].rearrange("p t (c i) -> p c t i", i=LINE),
                )

        def quantize_wf():
            for lo, hi in ((0, WF_SPLIT), (WF_SPLIT, H_PASSES * N)):
                quantize(wf_codes[:, lo:hi], wf_sc[:, lo:hi], wf_bf[:, lo * PACK : hi * PACK])

        def order_we(g):
            (nc.vector, nc.gpsimd)[g].tensor_copy(
                out=we_codes[g][:].bitcast(I32).rearrange("p (a t b w) -> p a t b w", a=C_PASSES, t=PACK, w=4),
                in_=we_raw[g][:].rearrange("p a (b t w) -> p a t b w", t=PACK, w=4),
            )

        def order_we_scales(g):
            words = PASS // 4
            (nc.vector, nc.gpsimd)[g].tensor_copy(
                out=we_sc[g][:].bitcast(I32).rearrange("p (a t b w) -> p a t b w", a=C_PASSES, t=PACK, w=2),
                in_=we_s_raw[:, :, g * words : (g + 1) * words].rearrange("p a (b t w) -> p a t b w", t=PACK, w=2),
            )

        def gather_tab(a, lo, hi):
            nc.vector.tensor_copy(
                v_codes[a][:, lo * QW : hi * QW],
                tab_w[a][:].bitcast(U32).indirect(tab_list[:, lo * LIST_COLS : hi * LIST_COLS]),
            )

        def square(u):
            q, g = u
            for u2 in range(PACK // 2):
                bank = take(first_ring if g == 0 else py_ring)[:].rearrange("p (t n) -> p t n", t=2)
                for t2 in range(2):
                    w = slice((2 * u2 + t2) * P, (2 * u2 + t2 + 1) * P)
                    nc.tensor.matmul_mx(
                        out=bank[:, t2, :],
                        lhsT=wp_codes[g][:, w].bitcast(FP8X4),
                        lhsT_scale=wp_sc[g][:, w],
                        rhs=xg_codes[q][:].bitcast(FP8X4),
                        rhs_scale=xg_sc[q][:],
                        start=True,
                        stop=True,
                    )
                nc.scalar.activation(
                    out=sq[u][:, u2 * PASS : (u2 + 1) * PASS], in_=bank.rearrange("p t n -> p (t n)"), func=ACT.Square
                )

        done = []

        def subtract(u, c):
            q, g = u
            whole = take(e_ring)
            bank = whole[:].rearrange("p (t n) -> p t n", t=PACK)
            cols = slice(q * QW + c * P, q * QW + (c + 1) * P)
            for a in range(C_PASSES):
                for t in range(PACK):
                    lo = (a * PACK + t) * P
                    nc.tensor.matmul_mx(
                        out=bank[:, t, :],
                        lhsT=we_codes[g][:, 2 * lo : 2 * (lo + P)].bitcast(FP4X4),
                        lhsT_scale=we_sc[g][:, lo : lo + P],
                        rhs=v_codes[a][:, cols].bitcast(FP8X4),
                        rhs_scale=v_scales[a][:, cols],
                        start=(a == 0 and t == 0),
                        stop=(a == C_PASSES - 1 and t == PACK - 1),
                    )
            part = slice(c * PASS, (c + 1) * PASS)
            nc.vector.tensor_tensor(
                h_bf[u][:, part].rearrange("p (n i t) -> p n t i", t=PACK, i=PAIR),
                sq[u][:].rearrange("p (t c n i) -> p c n t i", t=PACK, c=CHUNKS, i=PAIR)[:, c],
                bank[:].rearrange("p t (n i) -> p n t i", i=PAIR),
                ALU.subtract,
            )
            done.append(whole)
            if len(done) > len(units) * CHUNKS - E_BANKS:
                py_ring.insert(0, whole)

        def clamp(u, lo, hi):
            part = h_bf[u][:, lo * PACK : hi * PACK]
            nc.vector.tensor_scalar_max(part, part, 0.0)

        def force(q, lo, hi):
            for s in range(N_SLICES):
                bank = take(py_ring)[:, 0 : hi - lo]
                for g in range(H_PASSES):
                    w = slice(g * N + s * P, g * N + (s + 1) * P)
                    nc.tensor.matmul_mx(
                        out=bank[:],
                        lhsT=wf_codes[:, w].bitcast(FP8X4),
                        lhsT_scale=wf_sc[:, w],
                        rhs=h_codes[(q, g)][:, lo:hi].bitcast(FP8X4),
                        rhs_scale=h_sc[(q, g)][:, lo:hi],
                        start=(g == 0),
                        stop=(g == H_PASSES - 1),
                    )
                if q == QUARTERS - 1 and hi == QW and s % 2 == 0:
                    nc.vector.tensor_scalar_add(y_sb[q][:, s, lo:hi], bank[:], bias[:, s : s + 1])
                else:
                    nc.scalar.activation(
                        out=y_sb[q][:, s, lo:hi], in_=bank[:], func=ACT.Identity, bias=bias[:, s : s + 1]
                    )
            nc.sync.dma_start(
                out=out.rearrange("(s p) j -> p s j", p=P)[:, :, q * QW + lo : q * QW + hi],
                in_=y_sb[q][:, :, lo:hi],
            )

        def finish(u, lo, hi):
            q, g = u
            quantize(h_codes[u][:, lo:hi], h_sc[u][:, lo:hi], h_bf[u][:, lo * PACK : hi * PACK])
            if g == H_PASSES - 1:
                force(q, lo, hi)

        nc.vector.memset(tab_s[32:64, :].bitcast(I32), 0)
        nc.vector.memset(tab_s[64:128, :].bitcast(I32), 0)
        nc.vector.memset(we_s_raw[:], 0)
        for a in range(C_PASSES):
            nc.vector.memset(v_scales[a][:].bitcast(I32), 0)

        make_identity(nc, ident[:])
        nc.sync.dma_start(
            out=tab_s[0:32, :].bitcast(I32), in_=tab_scales.rearrange("a q t -> (a q) t").bitcast(I32)
        )
        nc.sync.dma_start(out=tab_list[:], in_=offs)
        nc.vector.tensor_copy(picked_s[:], tab_s[:].indirect(tab_list[:]))
        load_wgt()
        nc.sync.dma_start(out=edge_list[:], in_=offs2)

        load_x(0)
        spread_wgt()
        load_x(1)
        load_x(2)
        load_x(3)
        load_wp(0)
        load_tab(0)
        move_scales(0)
        load_we(0)
        load_we_scales()
        load_tab(1)
        move_scales(1)
        load_we(1)
        load_wp(1)
        for g in range(H_PASSES):
            load_wf(g)
        with nc.allow_non_contiguous_dma(reason="one bias value a partition"):
            nc.sync.dma_start(out=bias[:], in_=load.rearrange("(s p) -> p s", p=P))

        gather_x(0, 0, 1)
        gather_x(0, 1, 2)
        gather_x(0, 2, QUARTERS)
        for i in range(1, PACK - 1):
            gather_x(i, 0, QUARTERS)
        x_order = [0, 1, 2, 3]
        gather_x(PACK - 1, 0, 1)
        gather_x(PACK - 1, 1, 2)
        gather_x(PACK - 1, 2, QUARTERS)
        for q in x_order:
            if q == 1:
                prepare_wp(0)
            prepare_x(q)
        for q in x_order:
            if q == 3:
                prepare_wp(1)
            square((q, 0))
        gather_tab(0, 0, 2)
        order_we_scales(0)
        order_we(0)
        order_we_scales(1)
        gather_tab(0, 2, QUARTERS)
        gather_tab(1, 0, 1)
        gather_tab(1, 1, 2)
        gather_tab(1, 2, QUARTERS)
        order_we(1)
        square((0, 1))
        square((1, 1))
        weave_wf(0)
        weave_wf(1)
        quantize_wf()
        square((2, 1))
        square((3, 1))

        steps = [(0, 0, 0, QW), (1, 0, 0, QW), (2, 0, 0, QW), (0, 1, 0, QW), (1, 1, 0, QW), (2, 1, 0, QW), (3, 0, 0, P), (3, 1, 0, P), (3, 0, P, QW), (3, 1, P, QW)]
        behind = []
        for q, g, lo, hi in steps:
            u = (q, g)
            for c in range(lo // P, hi // P):
                subtract(u, c)
                if behind:
                    step, args = behind.pop(0)
                    step(*args)
            behind.extend([(clamp, (u, lo, hi)), (finish, (u, lo, hi))])
            while len(behind) > 3:
                step, args = behind.pop(0)
                step(*args)
        for step, args in behind:
            step(*args)
